import numpy as np
import ml_dtypes


def mxq(x, axis, fmt="e4m3"):
    dtype, down = {"e4m3": (ml_dtypes.float8_e4m3fn, 7), "e5m2": (ml_dtypes.float8_e5m2, 14)}[fmt]
    v = np.moveaxis(np.asarray(x, np.float32).astype(ml_dtypes.bfloat16).astype(np.float64), axis, -1)
    blocks = v.reshape(v.shape[:-1] + (-1, 32))
    amax = np.abs(blocks).max(-1, keepdims=True)
    byte = np.maximum(np.where(amax > 0, np.frexp(amax)[1] - 1 + 127, 0) - down, 1)
    scale = np.exp2(byte - 127.0)
    codes = (blocks / scale).astype(np.float32).astype(dtype).astype(np.float64)
    return np.moveaxis((codes * scale).reshape(v.shape), -1, axis)


WIDE = False


def mx_kscale(k):
    if not WIDE:
        return np.ones(k)
    levels = np.array([10, -10, 5, -5, 0])
    if k % 512:
        return np.exp2(np.random.permutation(np.resize(levels, k // 32))).repeat(32)
    a = np.empty((k // 512, 16))
    for p in range(k // 512):
        a[p, :8] = np.random.permutation(np.resize(levels, 8))
        for g in range(8):
            far = levels[np.abs(levels - a[p, g]) >= 10]
            a[p, g + 8] = far[np.random.randint(len(far))]
    return np.exp2(a.ravel()).repeat(32)


def f64(x):
    return np.asarray(x).astype(np.float64)


def striped(idx):
    return np.tile(idx.reshape(-1, 16).T, (8, 1)).astype(np.uint16)


def unstriped(offs):
    return offs[:16].T.reshape(-1).astype(np.int64)


E2M1 = np.array([0.0, 0.5, 1.0, 1.5, 2.0, 3.0, 4.0, 6.0, -0.0, -0.5, -1.0, -1.5, -2.0, -3.0, -4.0, -6.0])


def pack_weight(w, fmt):
    k, n = w.shape
    w = f64(np.asarray(w, np.float32).astype(ml_dtypes.bfloat16)).reshape(k // 32, 32, n)
    amax = np.abs(w).max(1)
    if fmt == "e4m3":
        byte = np.frexp(amax)[1] - 1 + 127 - 7
    else:
        mant, ex = np.frexp(amax / 6.0)
        byte = np.where(mant > 0.5, ex, ex - 1) + 127
    byte = np.clip(np.where(amax > 0, byte, 1), 1, 254)
    scaled = (w * np.exp2(127.0 - byte)[:, None, :]).reshape(k, n).astype(np.float32)
    by_word = np.ascontiguousarray(scaled.reshape(k // 512, 128, 4, n).transpose(0, 1, 3, 2))
    if fmt == "e4m3":
        words = by_word.astype(ml_dtypes.float8_e4m3fn).view(np.uint8)
    else:
        c = by_word.astype(ml_dtypes.float4_e2m1fn).view(np.uint8) & 0xF
        words = (c[..., 0::2] | (c[..., 1::2] << 4)).reshape(k // 512, 128, 2 * n)
    return np.ascontiguousarray(words), np.ascontiguousarray(byte.astype(np.uint8).reshape(k // 512, 16, n))


def unpack_weight(words, scales, fmt):
    g, _, n = scales.shape
    words = np.ascontiguousarray(words).reshape(g, 128, n, -1)
    if fmt == "e4m3":
        vals = words.view(ml_dtypes.float8_e4m3fn).astype(np.float64)
    else:
        nib = np.empty((g, 128, n, 4), np.uint8)
        nib[..., 0::2] = words & 0xF
        nib[..., 1::2] = words >> 4
        vals = E2M1[nib]
    vals = vals * np.repeat(np.exp2(scales.astype(np.float64) - 127.0), 8, axis=1)[..., None]
    return vals.transpose(0, 1, 3, 2).reshape(g * 512, n)


def relu(v):
    return np.maximum(v, 0.0)


K, T, Q, E, C, D, H = 1024, 1024, 768, 4, 128, 128, 0
N = 256


def by_expert(wq, xq, C):
    return np.concatenate([wq[e].T @ xq[:, e * C:(e + 1) * C] for e in range(E)], axis=1)


def setup_inputs():
    n = np.random.standard_normal
    s = mx_kscale(K)
    slot_token = np.random.permutation(T)[:E * C]
    slots2 = np.concatenate([np.random.permutation(Q)[:D] for e in range(E)])
    x = pack_weight(n((K, Q)) * s[:, None], "e4m3")
    return {
        "x_words": x[0],
        "x_scales": x[1],
        "xo": (n((K, T)) * s[:, None]).astype(np.float32),
        "w": (n((E, K, N)) / np.sqrt(K) / s[None, :, None]).astype(np.float32),
        "gate": np.tile(np.random.uniform(0.2, 1.0, E * C), (128, 1)).astype(np.float32),
        "offs": striped(slot_token),
        "offs2": striped(slots2),
    }


def reference(x_words, x_scales, xo, w, gate, offs, offs2):
    wq = mxq(f64(w), 1, "e4m3")
    idx, idx2 = unstriped(offs), unstriped(offs2)
    xq = mxq(f64(xo)[:, idx], 0, "e4m3")
    rq = unpack_weight(x_words, x_scales, "e4m3")[:, idx2]
    y = relu(by_expert(wq, xq, C))
    z = relu(by_expert(wq, rq, D))
    own = np.zeros((N, T))
    own[:, idx] = f64(gate[:1]) * y
    return np.concatenate([own, z], axis=1)

@@ -1,0 +1,183 @@
+from contextlib import ExitStack
+
+import concourse.mybir as mybir
+
+K, T, Q, E, C, N = 1024, 1024, 768, 4, 128, 256
+SLOTS = E * C
+FLOPS = 2 * 2 * SLOTS * K * N
+
+F32 = mybir.dt.float32
+BF16 = mybir.dt.bfloat16
+I32 = mybir.dt.int32
+U32 = mybir.dt.uint32
+U16 = mybir.dt.uint16
+U8 = mybir.dt.uint8
+FP8X4 = mybir.dt.float8_e4m3fn_x4
+COPY = mybir.ActivationFunctionType.Copy
+RELU = mybir.ActivationFunctionType.Relu
+MULT = mybir.AluOpType.mult
+
+P = 128
+PACK = 4
+K_PASS = P * PACK
+PASSES = K // K_PASS
+BLOCKS = N // P
+HALF = T // 2
+X_VECTOR_SHARE = {(0, 0, 1): HALF, (1, 1, 1): 320}
+W_VECTOR_SHARE = {}
+
+
+def tile_moe_loc_lin_relu_kernel(tc, x_words, x_scales, xo, w, gate, offs, offs2, out):
+    nc = tc.nc
+    with ExitStack() as ctx:
+        lists = ctx.enter_context(tc.tile_pool(name="lists", bufs=1))
+        keep = ctx.enter_context(tc.tile_pool(name="keep", bufs=1))
+        psum = ctx.enter_context(tc.psum_pool(name="psum", bufs=1))
+
+        own_list = lists.tile([P, SLOTS // 16], U16, name="own_list")
+        far_list = lists.tile([P, SLOTS // 16], U16, name="far_list")
+
+        far_words = [keep.tile([P, Q], I32, name="far_words%d" % s, align_bytes=64) for s in range(PASSES)]
+        far_bytes = keep.tile([P, Q], U8, name="far_bytes", align_bytes=64)
+        far_codes = [keep.tile([P, SLOTS], U32, name="far_codes%d" % s, align_bytes=64) for s in range(PASSES)]
+        far_scales = keep.tile([P, SLOTS], U8, name="far_scales", align_bytes=64)
+        own_out = [keep.tile([P, T], F32, name="own_out%d" % b, align_bytes=64) for b in range(BLOCKS)]
+        far_out = keep.tile([P, BLOCKS, SLOTS], F32, name="far_out", align_bytes=64)
+        gate_sb = keep.tile([P, SLOTS], F32, name="gate_sb", align_bytes=64)
+
+        nc.vector.memset(far_bytes[:].bitcast(I32), 0)
+        for b in range(BLOCKS):
+            nc.gpsimd.memset(own_out[b][:], 0.0)
+
+        def load_words(s):
+            nc.sync.dma_start(out=far_words[s][:], in_=x_words[s].rearrange("p t d -> p (t d)").bitcast(I32))
+
+        x_raw = {}
+
+        def load_x(s, u):
+            rows = xo[s * K_PASS:(s + 1) * K_PASS, :].rearrange("(p j) t -> p j t", j=PACK)
+            for h in range(2):
+                x_raw[s, u, h] = keep.tile([P, 2, HALF], F32, name="x_raw%d%d%d" % (s, u, h), align_bytes=64)
+                nc.sync.dma_start(out=x_raw[s, u, h][:], in_=rows[:, 2 * u:2 * u + 2, h * HALF:(h + 1) * HALF])
+
+        w_raw = {}
+
+        def load_w(e, s):
+            w_raw[e, s] = keep.tile([P, PACK, N], F32, name="w_raw%d%d" % (e, s), align_bytes=64)
+            nc.sync.dma_start(out=w_raw[e, s][:], in_=w[e, s * K_PASS:(s + 1) * K_PASS, :].rearrange("(p j) n -> p j n", j=PACK))
+
+        nc.sync.dma_start(far_list[:], offs2)
+        load_words(0)
+        load_x(0, 0)
+        nc.sync.dma_start(own_list[:], offs)
+        scale_rows = x_scales.bitcast(I32)
+        for q in range(4):
+            nc.sync.dma_start(out=far_bytes[32 * q:32 * q + 4 * PASSES, :].bitcast(I32), in_=scale_rows[:, 4 * q:4 * q + 4, :])
+        load_x(0, 1)
+        load_x(1, 0)
+        load_x(1, 1)
+        for e in range(E):
+            for s in range(PASSES):
+                load_w(e, s)
+            if e == 0:
+                load_words(1)
+                nc.sync.dma_start(out=gate_sb[:], in_=gate)
+
+        def gather_words(s):
+            nc.vector.tensor_copy(far_codes[s][:], far_words[s][:].bitcast(U32).indirect(far_list[:]))
+
+        own_codes = [keep.tile([P, SLOTS], U32, name="own_codes%d" % s, align_bytes=64) for s in range(PASSES)]
+        own_scales = [keep.tile([P, SLOTS], U8, name="own_scales%d" % s, align_bytes=64) for s in range(PASSES)]
+        woven = [keep.tile([P, PACK * SLOTS], BF16, name="woven%d" % s, align_bytes=64) for s in range(PASSES)]
+
+        def pick(s, u):
+            pairs = keep.tile([P, 2 * T], BF16, name="pairs%d%d" % (s, u), align_bytes=64)
+            for h in range(2):
+                dst = pairs[:, 2 * h * HALF:2 * (h + 1) * HALF].rearrange("p (t d) -> p t d", d=2)
+                src = x_raw[s, u, h][:].rearrange("p d t -> p t d")
+                cut = X_VECTOR_SHARE.get((s, u, h), 0)
+                if cut > 0:
+                    nc.vector.tensor_copy(dst[:, :cut], src[:, :cut])
+                if cut < HALF:
+                    nc.scalar.activation(dst[:, cut:], src[:, cut:], COPY)
+            words = woven[s][:].bitcast(U32).rearrange("p (j u) -> p j u", u=2)
+            nc.vector.tensor_copy(words[:, :, u], pairs[:].bitcast(U32).indirect(own_list[:]))
+
+        def quantize_x(s):
+            nc.vector.quantize_mx(out=own_codes[s][:].bitcast(FP8X4), scales=own_scales[s][:], in_=woven[s][:])
+
+        gather_words(0)
+        nc.vector.tensor_copy(far_scales[:], far_bytes[:].indirect(far_list[:]))
+        pick(0, 0)
+        pick(0, 1)
+        quantize_x(0)
+        pick(1, 0)
+        pick(1, 1)
+        quantize_x(1)
+
+        w_codes, w_scales = {}, {}
+
+        def prepare_w(e, s):
+            grouped = keep.tile([P, PACK * N], BF16, name="w_grouped%d%d" % (e, s), align_bytes=64)
+            src = w_raw[e, s][:].rearrange("p j (c i) -> p c j i", i=4)
+            dst = grouped[:].rearrange("p (c i j) -> p c j i", i=4, j=PACK)
+            cut = W_VECTOR_SHARE.get((e, s), 0) // 4
+            if cut > 0:
+                nc.vector.tensor_copy(dst[:, :cut], src[:, :cut])
+            nc.scalar.activation(dst[:, cut:], src[:, cut:], COPY)
+            w_codes[e, s] = keep.tile([P, N], U32, name="w_codes%d%d" % (e, s), align_bytes=64)
+            w_scales[e, s] = keep.tile([P, N], U8, name="w_scales%d%d" % (e, s), align_bytes=64)
+            nc.vector.quantize_mx(out=w_codes[e, s][:].bitcast(FP8X4), scales=w_scales[e, s][:], in_=grouped[:])
+
+        def multiply(acc, e, b, s, codes, scales):
+            cols = slice(b * P, (b + 1) * P)
+            nc.tensor.matmul_mx(
+                out=acc,
+                lhsT=w_codes[e, s][:, cols].bitcast(FP8X4),
+                lhsT_scale=w_scales[e, s][:, cols],
+                rhs=codes[:, e * C:(e + 1) * C].bitcast(FP8X4),
+                rhs_scale=scales[:, e * C:(e + 1) * C],
+                start=(s == 0),
+                stop=(s == PASSES - 1),
+            )
+
+        own_banks = {}
+
+        def multiply_own(e, s):
+            for b in range(BLOCKS):
+                if s == 0:
+                    own_banks[e, b] = psum.tile([P, C], F32, name="own_bank%d" % b, bufs=2)
+                multiply(own_banks[e, b][:], e, b, s, own_codes[s], own_scales[s])
+
+        def scatter(e, b):
+            y = keep.tile([P, C], F32, name="y%d%d" % (e, b), align_bytes=64)
+            nc.scalar.activation(y[:], own_banks[e, b][:], RELU)
+            entries = own_list[:, e * C // 16:(e + 1) * C // 16]
+            nc.vector.tensor_tensor(own_out[b][:].indirect(entries), y[:], gate_sb[:, e * C:(e + 1) * C], MULT)
+
+        def finish_far(e):
+            bank = psum.tile([P, BLOCKS, C], F32, name="far_bank%d" % e)
+            for b in range(BLOCKS):
+                for s in range(PASSES):
+                    multiply(bank[:, b, :], e, b, s, far_codes[s], far_scales[4 * s:P, :])
+            nc.scalar.activation(far_out[:, :, e * C:(e + 1) * C], bank[:], RELU)
+
+        out_rows = out.rearrange("(b p) c -> p b c", p=P)
+        for e in range(E):
+            for s in range(PASSES):
+                prepare_w(e, s)
+                if e > 0:
+                    scatter(e - 1, s)
+                multiply_own(e, s)
+            if e == 0:
+                gather_words(1)
+        for b in range(BLOCKS):
+            scatter(E - 1, b)
+        early = (E - 1) * C
+        for e in range(E - 1):
+            finish_far(e)
+        nc.sync.dma_start(out=out_rows[:, :, T:T + early], in_=far_out[:, :, :early])
+        finish_far(E - 1)
+        nc.sync.dma_start(out=out_rows[:, 0, :T], in_=own_out[0][:])
+        nc.sync.dma_start(out=out_rows[:, :, T + early:], in_=far_out[:, :, early:])
+        nc.sync.dma_start(out=out_rows[:, 1, :T], in_=own_out[1][:])

@@ -23,7 +23,7 @@ K_PASS = P * PACK
 PASSES = K // K_PASS
 BLOCKS = N // P
 HALF = T // 2
-X_VECTOR_SHARE = {(0, 0, 1): HALF, (1, 1, 1): 320}
+X_VECTOR_SHARE = {(1, 1, 1): 320}
 W_VECTOR_SHARE = {}
 
 
@@ -42,10 +42,9 @@ def tile_moe_loc_lin_relu_kernel(tc, x_words, x_scales, xo, w, gate, offs, offs2
         far_codes = [keep.tile([P, SLOTS], U32, name="far_codes%d" % s, align_bytes=64) for s in range(PASSES)]
         far_scales = keep.tile([P, SLOTS], U8, name="far_scales", align_bytes=64)
         own_out = [keep.tile([P, T], F32, name="own_out%d" % b, align_bytes=64) for b in range(BLOCKS)]
-        far_out = keep.tile([P, BLOCKS, SLOTS], F32, name="far_out", align_bytes=64)
         gate_sb = keep.tile([P, SLOTS], F32, name="gate_sb", align_bytes=64)
 
-        nc.vector.memset(far_bytes[:].bitcast(I32), 0)
+        nc.gpsimd.memset(far_bytes[:].bitcast(I32), 0)
         for b in range(BLOCKS):
             nc.gpsimd.memset(own_out[b][:], 0.0)
 
@@ -63,34 +62,48 @@ def tile_moe_loc_lin_relu_kernel(tc, x_words, x_scales, xo, w, gate, offs, offs2
         w_raw = {}
 
         def load_w(e, s):
-            w_raw[e, s] = keep.tile([P, PACK, N], F32, name="w_raw%d%d" % (e, s), align_bytes=64)
+            w_raw[e, s] = keep.tile([P, PACK, N], F32, name="w_raw%d%d" % (e, s), tag="w_raw%d%d" % (e, s), align_bytes=64)
             nc.sync.dma_start(out=w_raw[e, s][:], in_=w[e, s * K_PASS:(s + 1) * K_PASS, :].rearrange("(p j) n -> p j n", j=PACK))
+
+        def load_scales():
+            scale_rows = x_scales.bitcast(I32)
+            for q in range(4):
+                nc.sync.dma_start(out=far_bytes[32 * q:32 * q + 4 * PASSES, :].bitcast(I32), in_=scale_rows[:, 4 * q:4 * q + 4, :])
+
+        def load_gate(e0, e1):
+            nc.sync.dma_start(out=gate_sb[:, e0 * C:e1 * C], in_=gate[:, e0 * C:e1 * C])
 
         nc.sync.dma_start(far_list[:], offs2)
         load_words(0)
         load_x(0, 0)
         nc.sync.dma_start(own_list[:], offs)
-        scale_rows = x_scales.bitcast(I32)
-        for q in range(4):
-            nc.sync.dma_start(out=far_bytes[32 * q:32 * q + 4 * PASSES, :].bitcast(I32), in_=scale_rows[:, 4 * q:4 * q + 4, :])
+        load_scales()
+        load_words(1)
         load_x(0, 1)
         load_x(1, 0)
         load_x(1, 1)
-        for e in range(E):
-            for s in range(PASSES):
-                load_w(e, s)
-            if e == 0:
-                load_words(1)
-                nc.sync.dma_start(out=gate_sb[:], in_=gate)
+        load_w(0, 0)
+        load_w(0, 1)
+        load_w(1, 0)
+        load_gate(0, 2)
+        load_w(1, 1)
+        load_w(2, 0)
+        load_w(2, 1)
+        load_w(3, 0)
+        load_w(3, 1)
+        load_gate(2, E)
 
         def gather_words(s):
             nc.vector.tensor_copy(far_codes[s][:], far_words[s][:].bitcast(U32).indirect(far_list[:]))
 
+        picked = [keep.tile([P, 2, SLOTS], U32, name="picked%d" % s, align_bytes=64) for s in range(PASSES)]
         own_codes = [keep.tile([P, SLOTS], U32, name="own_codes%d" % s, align_bytes=64) for s in range(PASSES)]
         own_scales = [keep.tile([P, SLOTS], U8, name="own_scales%d" % s, align_bytes=64) for s in range(PASSES)]
         woven = [keep.tile([P, PACK * SLOTS], BF16, name="woven%d" % s, align_bytes=64) for s in range(PASSES)]
 
-        def pick(s, u):
+        pair_tiles = {}
+
+        def cast_x(s, u):
             pairs = keep.tile([P, 2 * T], BF16, name="pairs%d%d" % (s, u), align_bytes=64)
             for h in range(2):
                 dst = pairs[:, 2 * h * HALF:2 * (h + 1) * HALF].rearrange("p (t d) -> p t d", d=2)
@@ -100,20 +113,36 @@ def tile_moe_loc_lin_relu_kernel(tc, x_words, x_scales, xo, w, gate, offs, offs2
                     nc.vector.tensor_copy(dst[:, :cut], src[:, :cut])
                 if cut < HALF:
                     nc.scalar.activation(dst[:, cut:], src[:, cut:], COPY)
-            words = woven[s][:].bitcast(U32).rearrange("p (j u) -> p j u", u=2)
-            nc.vector.tensor_copy(words[:, :, u], pairs[:].bitcast(U32).indirect(own_list[:]))
+            pair_tiles[s, u] = pairs
 
-        def quantize_x(s):
-            nc.vector.quantize_mx(out=own_codes[s][:].bitcast(FP8X4), scales=own_scales[s][:], in_=woven[s][:])
+        def pick(s, u, j0, j1):
+            nc.vector.tensor_copy(picked[s][:, u, j0:j1], pair_tiles[s, u][:].bitcast(U32).indirect(own_list[:, j0 // 16:j1 // 16]))
+
+        def weave(s, j0, j1):
+            words = woven[s][:].bitcast(I32).rearrange("p (j u) -> p j u", u=2)
+            nc.vector.tensor_copy(words[:, j0:j1, :], picked[s][:].bitcast(I32).rearrange("p u j -> p j u")[:, j0:j1, :])
+
+        def quantize_x(s, j0, j1):
+            nc.vector.quantize_mx(out=own_codes[s][:, j0:j1].bitcast(FP8X4), scales=own_scales[s][:, j0:j1], in_=woven[s][:, PACK * j0:PACK * j1])
+
+        def gather_scales():
+            nc.vector.tensor_copy(far_scales[:], far_bytes[:].indirect(far_list[:]))
 
         gather_words(0)
-        nc.vector.tensor_copy(far_scales[:], far_bytes[:].indirect(far_list[:]))
-        pick(0, 0)
-        pick(0, 1)
-        quantize_x(0)
-        pick(1, 0)
-        pick(1, 1)
-        quantize_x(1)
+        gather_scales()
+        cast_x(0, 0)
+        pick(0, 0, 0, SLOTS)
+        gather_words(1)
+        cast_x(0, 1)
+        pick(0, 1, 0, SLOTS)
+        cast_x(1, 0)
+        weave(0, 0, SLOTS)
+        quantize_x(0, 0, SLOTS)
+        pick(1, 0, 0, SLOTS)
+        cast_x(1, 1)
+        pick(1, 1, 0, SLOTS // 2)
+        weave(1, 0, SLOTS // 2)
+        quantize_x(1, 0, SLOTS // 2)
 
         w_codes, w_scales = {}, {}
 
@@ -126,8 +155,11 @@ def tile_moe_loc_lin_relu_kernel(tc, x_words, x_scales, xo, w, gate, offs, offs2
                 nc.vector.tensor_copy(dst[:, :cut], src[:, :cut])
             nc.scalar.activation(dst[:, cut:], src[:, cut:], COPY)
             w_codes[e, s] = keep.tile([P, N], U32, name="w_codes%d%d" % (e, s), align_bytes=64)
-            w_scales[e, s] = keep.tile([P, N], U8, name="w_scales%d%d" % (e, s), align_bytes=64)
-            nc.vector.quantize_mx(out=w_codes[e, s][:].bitcast(FP8X4), scales=w_scales[e, s][:], in_=grouped[:])
+            if s == 0 and e > 0:
+                w_scales[e, s] = w_scales[e - 1, 1][4:P, :]
+            else:
+                w_scales[e, s] = keep.tile([P, N], U8, name="w_scales%d%d" % (e, s), align_bytes=64)[:]
+            nc.vector.quantize_mx(out=w_codes[e, s][:].bitcast(FP8X4), scales=w_scales[e, s], in_=grouped[:])
 
         def multiply(acc, e, b, s, codes, scales):
             cols = slice(b * P, (b + 1) * P)
@@ -143,11 +175,10 @@ def tile_moe_loc_lin_relu_kernel(tc, x_words, x_scales, xo, w, gate, offs, offs2
 
         own_banks = {}
 
-        def multiply_own(e, s):
-            for b in range(BLOCKS):
-                if s == 0:
-                    own_banks[e, b] = psum.tile([P, C], F32, name="own_bank%d" % b, bufs=2)
-                multiply(own_banks[e, b][:], e, b, s, own_codes[s], own_scales[s])
+        def multiply_own(e, b, s):
+            if s == 0:
+                own_banks[e, b] = psum.tile([P, C], F32, name="own_bank%d" % b, bufs=2)
+            multiply(own_banks[e, b][:], e, b, s, own_codes[s], own_scales[s])
 
         def scatter(e, b):
             y = keep.tile([P, C], F32, name="y%d%d" % (e, b), align_bytes=64)
@@ -167,12 +198,19 @@ def tile_moe_loc_lin_relu_kernel(tc, x_words, x_scales, xo, w, gate, offs, offs2
             for s in range(PASSES):
                 prepare_w(e, s)
                 if e > 0:
+                    if s == 0:
+                        multiply_own(e - 1, 1, 1)
                     scatter(e - 1, s)
-                multiply_own(e, s)
-            if e == 0:
-                gather_words(1)
+                multiply_own(e, 0, s)
+                if s == 0 or e == E - 1:
+                    multiply_own(e, 1, s)
+                if (e, s) == (0, 1):
+                    pick(1, 1, SLOTS // 2, SLOTS)
+                    weave(1, SLOTS // 2, SLOTS)
+                    quantize_x(1, SLOTS // 2, SLOTS)
         for b in range(BLOCKS):
             scatter(E - 1, b)
+        far_out = keep.tile([P, BLOCKS, SLOTS], F32, name="far_out", tag="w_raw31", align_bytes=64)
         early = (E - 1) * C
         for e in range(E - 1):
             finish_far(e)

@@ -22,9 +22,13 @@ PACK = 4
 K_PASS = P * PACK
 PASSES = K // K_PASS
 BLOCKS = N // P
-HALF = T // 2
-X_VECTOR_SHARE = {(1, 1, 1): 320}
-W_VECTOR_SHARE = {}
+QUADRANTS = 4
+SCALE_ROWS = 4
+PER_COLUMN = 16
+HALF_T = T // 2
+HALF_SLOTS = SLOTS // 2
+LAST_CAST_ON_VECTOR = 192
+WALK = 2
 
 
 def tile_moe_loc_lin_relu_kernel(tc, x_words, x_scales, xo, w, gate, offs, offs2, out):
@@ -34,8 +38,8 @@ def tile_moe_loc_lin_relu_kernel(tc, x_words, x_scales, xo, w, gate, offs, offs2
         keep = ctx.enter_context(tc.tile_pool(name="keep", bufs=1))
         psum = ctx.enter_context(tc.psum_pool(name="psum", bufs=1))
 
-        own_list = lists.tile([P, SLOTS // 16], U16, name="own_list")
-        far_list = lists.tile([P, SLOTS // 16], U16, name="far_list")
+        own_list = lists.tile([P, SLOTS // PER_COLUMN], U16, name="own_list")
+        far_list = lists.tile([P, SLOTS // PER_COLUMN], U16, name="far_list")
 
         far_words = [keep.tile([P, Q], I32, name="far_words%d" % s, align_bytes=64) for s in range(PASSES)]
         far_bytes = keep.tile([P, Q], U8, name="far_bytes", align_bytes=64)
@@ -53,11 +57,20 @@ def tile_moe_loc_lin_relu_kernel(tc, x_words, x_scales, xo, w, gate, offs, offs2
 
         x_raw = {}
 
-        def load_x(s, u):
+        def x_rows(s, u):
             rows = xo[s * K_PASS:(s + 1) * K_PASS, :].rearrange("(p j) t -> p j t", j=PACK)
+            return rows[:, 2 * u:2 * u + 2, :]
+
+        def load_x_whole(s, u):
+            whole = keep.tile([P, 2, T], F32, name="x_raw%d%d" % (s, u), align_bytes=64)
+            nc.sync.dma_start(out=whole[:], in_=x_rows(s, u))
             for h in range(2):
-                x_raw[s, u, h] = keep.tile([P, 2, HALF], F32, name="x_raw%d%d%d" % (s, u, h), align_bytes=64)
-                nc.sync.dma_start(out=x_raw[s, u, h][:], in_=rows[:, 2 * u:2 * u + 2, h * HALF:(h + 1) * HALF])
+                x_raw[s, u, h] = whole[:, :, h * HALF_T:(h + 1) * HALF_T]
+
+        def load_x(s, u):
+            for h in range(2):
+                x_raw[s, u, h] = keep.tile([P, 2, HALF_T], F32, name="x_raw%d%d%d" % (s, u, h), align_bytes=64)[:]
+                nc.sync.dma_start(out=x_raw[s, u, h], in_=x_rows(s, u)[:, :, h * HALF_T:(h + 1) * HALF_T])
 
         w_raw = {}
 
@@ -67,31 +80,30 @@ def tile_moe_loc_lin_relu_kernel(tc, x_words, x_scales, xo, w, gate, offs, offs2
 
         def load_scales():
             scale_rows = x_scales.bitcast(I32)
-            for q in range(4):
-                nc.sync.dma_start(out=far_bytes[32 * q:32 * q + 4 * PASSES, :].bitcast(I32), in_=scale_rows[:, 4 * q:4 * q + 4, :])
+            for q in range(QUADRANTS):
+                nc.sync.dma_start(
+                    out=far_bytes[32 * q:32 * q + SCALE_ROWS * PASSES, :].bitcast(I32),
+                    in_=scale_rows[:, SCALE_ROWS * q:SCALE_ROWS * (q + 1), :],
+                )
 
         def load_gate(e0, e1):
             nc.sync.dma_start(out=gate_sb[:, e0 * C:e1 * C], in_=gate[:, e0 * C:e1 * C])
 
         nc.sync.dma_start(far_list[:], offs2)
         load_words(0)
-        load_x(0, 0)
+        load_x_whole(0, 0)
         nc.sync.dma_start(own_list[:], offs)
         load_scales()
         load_words(1)
         load_x(0, 1)
         load_x(1, 0)
         load_x(1, 1)
-        load_w(0, 0)
-        load_w(0, 1)
-        load_w(1, 0)
-        load_gate(0, 2)
-        load_w(1, 1)
-        load_w(2, 0)
-        load_w(2, 1)
-        load_w(3, 0)
-        load_w(3, 1)
-        load_gate(2, E)
+        for e in range(E):
+            for s in range(PASSES):
+                load_w(e, s)
+                if (e, s) == (1, 0):
+                    load_gate(0, E // 2)
+        load_gate(E // 2, E)
 
         def gather_words(s):
             nc.vector.tensor_copy(far_codes[s][:], far_words[s][:].bitcast(U32).indirect(far_list[:]))
@@ -101,35 +113,37 @@ def tile_moe_loc_lin_relu_kernel(tc, x_words, x_scales, xo, w, gate, offs, offs2
         own_scales = [keep.tile([P, SLOTS], U8, name="own_scales%d" % s, align_bytes=64) for s in range(PASSES)]
         woven = [keep.tile([P, PACK * SLOTS], BF16, name="woven%d" % s, align_bytes=64) for s in range(PASSES)]
 
-        pair_tiles = {}
+        pair_planes = {}
 
         def cast_x(s, u):
             pairs = keep.tile([P, 2 * T], BF16, name="pairs%d%d" % (s, u), align_bytes=64)
             for h in range(2):
-                dst = pairs[:, 2 * h * HALF:2 * (h + 1) * HALF].rearrange("p (t d) -> p t d", d=2)
-                src = x_raw[s, u, h][:].rearrange("p d t -> p t d")
-                cut = X_VECTOR_SHARE.get((s, u, h), 0)
-                if cut > 0:
+                dst = pairs[:, 2 * h * HALF_T:2 * (h + 1) * HALF_T].rearrange("p (t d) -> p t d", d=2)
+                src = x_raw[s, u, h].rearrange("p d t -> p t d")
+                cut = 0
+                if (s, u, h) == (PASSES - 1, 1, 1):
+                    cut = LAST_CAST_ON_VECTOR
                     nc.vector.tensor_copy(dst[:, :cut], src[:, :cut])
-                if cut < HALF:
-                    nc.scalar.activation(dst[:, cut:], src[:, cut:], COPY)
-            pair_tiles[s, u] = pairs
+                nc.scalar.activation(dst[:, cut:], src[:, cut:], COPY)
+            pair_planes[s, u] = pairs
 
         def pick(s, u, j0, j1):
-            nc.vector.tensor_copy(picked[s][:, u, j0:j1], pair_tiles[s, u][:].bitcast(U32).indirect(own_list[:, j0 // 16:j1 // 16]))
+            entries = own_list[:, j0 // PER_COLUMN:j1 // PER_COLUMN]
+            nc.vector.tensor_copy(picked[s][:, u, j0:j1], pair_planes[s, u][:].bitcast(U32).indirect(entries))
 
         def weave(s, j0, j1):
             words = woven[s][:].bitcast(I32).rearrange("p (j u) -> p j u", u=2)
             nc.vector.tensor_copy(words[:, j0:j1, :], picked[s][:].bitcast(I32).rearrange("p u j -> p j u")[:, j0:j1, :])
 
         def quantize_x(s, j0, j1):
-            nc.vector.quantize_mx(out=own_codes[s][:, j0:j1].bitcast(FP8X4), scales=own_scales[s][:, j0:j1], in_=woven[s][:, PACK * j0:PACK * j1])
-
-        def gather_scales():
-            nc.vector.tensor_copy(far_scales[:], far_bytes[:].indirect(far_list[:]))
+            nc.vector.quantize_mx(
+                out=own_codes[s][:, j0:j1].bitcast(FP8X4),
+                scales=own_scales[s][:, j0:j1],
+                in_=woven[s][:, PACK * j0:PACK * j1],
+            )
 
         gather_words(0)
-        gather_scales()
+        nc.vector.tensor_copy(far_scales[:], far_bytes[:].indirect(far_list[:]))
         cast_x(0, 0)
         pick(0, 0, 0, SLOTS)
         gather_words(1)
@@ -140,23 +154,20 @@ def tile_moe_loc_lin_relu_kernel(tc, x_words, x_scales, xo, w, gate, offs, offs2
         quantize_x(0, 0, SLOTS)
         pick(1, 0, 0, SLOTS)
         cast_x(1, 1)
-        pick(1, 1, 0, SLOTS // 2)
-        weave(1, 0, SLOTS // 2)
-        quantize_x(1, 0, SLOTS // 2)
+        pick(1, 1, 0, HALF_SLOTS)
+        weave(1, 0, HALF_SLOTS)
+        quantize_x(1, 0, HALF_SLOTS)
 
         w_codes, w_scales = {}, {}
 
         def prepare_w(e, s):
             grouped = keep.tile([P, PACK * N], BF16, name="w_grouped%d%d" % (e, s), align_bytes=64)
-            src = w_raw[e, s][:].rearrange("p j (c i) -> p c j i", i=4)
-            dst = grouped[:].rearrange("p (c i j) -> p c j i", i=4, j=PACK)
-            cut = W_VECTOR_SHARE.get((e, s), 0) // 4
-            if cut > 0:
-                nc.vector.tensor_copy(dst[:, :cut], src[:, :cut])
-            nc.scalar.activation(dst[:, cut:], src[:, cut:], COPY)
+            src = w_raw[e, s][:].rearrange("p j (c i) -> p c j i", i=WALK)
+            dst = grouped[:].rearrange("p (c i j) -> p c j i", i=WALK, j=PACK)
+            nc.scalar.activation(dst, src, COPY)
             w_codes[e, s] = keep.tile([P, N], U32, name="w_codes%d%d" % (e, s), align_bytes=64)
             if s == 0 and e > 0:
-                w_scales[e, s] = w_scales[e - 1, 1][4:P, :]
+                w_scales[e, s] = w_scales[e - 1, 1][SCALE_ROWS:P, :]
             else:
                 w_scales[e, s] = keep.tile([P, N], U8, name="w_scales%d%d" % (e, s), align_bytes=64)[:]
             nc.vector.quantize_mx(out=w_codes[e, s][:].bitcast(FP8X4), scales=w_scales[e, s], in_=grouped[:])
@@ -183,39 +194,43 @@ def tile_moe_loc_lin_relu_kernel(tc, x_words, x_scales, xo, w, gate, offs, offs2
         def scatter(e, b):
             y = keep.tile([P, C], F32, name="y%d%d" % (e, b), align_bytes=64)
             nc.scalar.activation(y[:], own_banks[e, b][:], RELU)
-            entries = own_list[:, e * C // 16:(e + 1) * C // 16]
+            entries = own_list[:, e * C // PER_COLUMN:(e + 1) * C // PER_COLUMN]
             nc.vector.tensor_tensor(own_out[b][:].indirect(entries), y[:], gate_sb[:, e * C:(e + 1) * C], MULT)
 
         def finish_far(e):
             bank = psum.tile([P, BLOCKS, C], F32, name="far_bank%d" % e)
             for b in range(BLOCKS):
                 for s in range(PASSES):
-                    multiply(bank[:, b, :], e, b, s, far_codes[s], far_scales[4 * s:P, :])
+                    multiply(bank[:, b, :], e, b, s, far_codes[s], far_scales[SCALE_ROWS * s:P, :])
             nc.scalar.activation(far_out[:, :, e * C:(e + 1) * C], bank[:], RELU)
 
+        last = E - 1
         out_rows = out.rearrange("(b p) c -> p b c", p=P)
         for e in range(E):
-            for s in range(PASSES):
-                prepare_w(e, s)
-                if e > 0:
-                    if s == 0:
-                        multiply_own(e - 1, 1, 1)
-                    scatter(e - 1, s)
-                multiply_own(e, 0, s)
-                if s == 0 or e == E - 1:
-                    multiply_own(e, 1, s)
-                if (e, s) == (0, 1):
-                    pick(1, 1, SLOTS // 2, SLOTS)
-                    weave(1, SLOTS // 2, SLOTS)
-                    quantize_x(1, SLOTS // 2, SLOTS)
+            prepare_w(e, 0)
+            if e > 0:
+                multiply_own(e - 1, 1, 1)
+                scatter(e - 1, 0)
+            multiply_own(e, 0, 0)
+            multiply_own(e, 1, 0)
+            prepare_w(e, 1)
+            if e > 0:
+                scatter(e - 1, 1)
+            multiply_own(e, 0, 1)
+            if e == 0:
+                pick(1, 1, HALF_SLOTS, SLOTS)
+                weave(1, HALF_SLOTS, SLOTS)
+                quantize_x(1, HALF_SLOTS, SLOTS)
+        multiply_own(last, 1, 1)
         for b in range(BLOCKS):
-            scatter(E - 1, b)
-        far_out = keep.tile([P, BLOCKS, SLOTS], F32, name="far_out", tag="w_raw31", align_bytes=64)
-        early = (E - 1) * C
-        for e in range(E - 1):
+            scatter(last, b)
+
+        far_out = keep.tile([P, BLOCKS, SLOTS], F32, name="far_out", tag="w_raw%d%d" % (last, PASSES - 1), align_bytes=64)
+        early = last * C
+        for e in range(last):
             finish_far(e)
         nc.sync.dma_start(out=out_rows[:, :, T:T + early], in_=far_out[:, :, :early])
-        finish_far(E - 1)
+        finish_far(last)
         nc.sync.dma_start(out=out_rows[:, 0, :T], in_=own_out[0][:])
         nc.sync.dma_start(out=out_rows[:, :, T + early:], in_=far_out[:, :, early:])
         nc.sync.dma_start(out=out_rows[:, 1, :T], in_=own_out[1][:])

@@ -27,7 +27,8 @@ SCALE_ROWS = 4
 PER_COLUMN = 16
 HALF_T = T // 2
 HALF_SLOTS = SLOTS // 2
-LAST_CAST_ON_VECTOR = 192
+VECTOR_SHARE = {(0, 1, 1): 256}
+W_SHARE = {}
 WALK = 2
 
 
@@ -61,15 +62,9 @@ def tile_moe_loc_lin_relu_kernel(tc, x_words, x_scales, xo, w, gate, offs, offs2
             rows = xo[s * K_PASS:(s + 1) * K_PASS, :].rearrange("(p j) t -> p j t", j=PACK)
             return rows[:, 2 * u:2 * u + 2, :]
 
-        def load_x_whole(s, u):
-            whole = keep.tile([P, 2, T], F32, name="x_raw%d%d" % (s, u), align_bytes=64)
-            nc.sync.dma_start(out=whole[:], in_=x_rows(s, u))
-            for h in range(2):
-                x_raw[s, u, h] = whole[:, :, h * HALF_T:(h + 1) * HALF_T]
-
         def load_x(s, u):
             for h in range(2):
-                x_raw[s, u, h] = keep.tile([P, 2, HALF_T], F32, name="x_raw%d%d%d" % (s, u, h), align_bytes=64)[:]
+                x_raw[s, u, h] = keep.tile([P, 2, HALF_T], F32, name="x_raw%d%d%d" % (s, u, h), tag="x_raw%d%d%d" % (s, u, h), align_bytes=64)[:]
                 nc.sync.dma_start(out=x_raw[s, u, h], in_=x_rows(s, u)[:, :, h * HALF_T:(h + 1) * HALF_T])
 
         w_raw = {}
@@ -89,12 +84,12 @@ def tile_moe_loc_lin_relu_kernel(tc, x_words, x_scales, xo, w, gate, offs, offs2
         def load_gate(e0, e1):
             nc.sync.dma_start(out=gate_sb[:, e0 * C:e1 * C], in_=gate[:, e0 * C:e1 * C])
 
-        nc.sync.dma_start(far_list[:], offs2)
         load_words(0)
-        load_x_whole(0, 0)
-        nc.sync.dma_start(own_list[:], offs)
-        load_scales()
+        nc.sync.dma_start(far_list[:], offs2)
         load_words(1)
+        load_scales()
+        load_x(0, 0)
+        nc.sync.dma_start(own_list[:], offs)
         load_x(0, 1)
         load_x(1, 0)
         load_x(1, 1)
@@ -109,9 +104,9 @@ def tile_moe_loc_lin_relu_kernel(tc, x_words, x_scales, xo, w, gate, offs, offs2
             nc.vector.tensor_copy(far_codes[s][:], far_words[s][:].bitcast(U32).indirect(far_list[:]))
 
         picked = [keep.tile([P, 2, SLOTS], U32, name="picked%d" % s, align_bytes=64) for s in range(PASSES)]
-        own_codes = [keep.tile([P, SLOTS], U32, name="own_codes%d" % s, align_bytes=64) for s in range(PASSES)]
+        own_codes = {1: keep.tile([P, SLOTS], U32, name="own_codes1", align_bytes=64)}
         own_scales = [keep.tile([P, SLOTS], U8, name="own_scales%d" % s, align_bytes=64) for s in range(PASSES)]
-        woven = [keep.tile([P, PACK * SLOTS], BF16, name="woven%d" % s, align_bytes=64) for s in range(PASSES)]
+        woven = {}
 
         pair_planes = {}
 
@@ -120,43 +115,46 @@ def tile_moe_loc_lin_relu_kernel(tc, x_words, x_scales, xo, w, gate, offs, offs2
             for h in range(2):
                 dst = pairs[:, 2 * h * HALF_T:2 * (h + 1) * HALF_T].rearrange("p (t d) -> p t d", d=2)
                 src = x_raw[s, u, h].rearrange("p d t -> p t d")
-                cut = 0
-                if (s, u, h) == (PASSES - 1, 1, 1):
-                    cut = LAST_CAST_ON_VECTOR
+                cut = VECTOR_SHARE.get((s, u, h), 0)
+                if cut:
                     nc.vector.tensor_copy(dst[:, :cut], src[:, :cut])
-                nc.scalar.activation(dst[:, cut:], src[:, cut:], COPY)
+                if cut < HALF_T:
+                    nc.scalar.activation(dst[:, cut:], src[:, cut:], COPY)
             pair_planes[s, u] = pairs
 
         def pick(s, u, j0, j1):
             entries = own_list[:, j0 // PER_COLUMN:j1 // PER_COLUMN]
             nc.vector.tensor_copy(picked[s][:, u, j0:j1], pair_planes[s, u][:].bitcast(U32).indirect(entries))
 
-        def weave(s, j0, j1):
-            words = woven[s][:].bitcast(I32).rearrange("p (j u) -> p j u", u=2)
-            nc.vector.tensor_copy(words[:, j0:j1, :], picked[s][:].bitcast(I32).rearrange("p u j -> p j u")[:, j0:j1, :])
+        def weave(s, j0, j1, tag):
+            woven[s, j0] = keep.tile([P, PACK * (j1 - j0)], BF16, name="woven%d_%d" % (s, j0), tag=tag, align_bytes=64)
+            words = woven[s, j0][:].bitcast(I32).rearrange("p (j u) -> p j u", u=2)
+            nc.vector.tensor_copy(words, picked[s][:].bitcast(I32).rearrange("p u j -> p j u")[:, j0:j1, :])
 
         def quantize_x(s, j0, j1):
             nc.vector.quantize_mx(
                 out=own_codes[s][:, j0:j1].bitcast(FP8X4),
                 scales=own_scales[s][:, j0:j1],
-                in_=woven[s][:, PACK * j0:PACK * j1],
+                in_=woven[s, j0][:],
             )
 
         gather_words(0)
+        gather_words(1)
         nc.vector.tensor_copy(far_scales[:], far_bytes[:].indirect(far_list[:]))
         cast_x(0, 0)
         pick(0, 0, 0, SLOTS)
-        gather_words(1)
         cast_x(0, 1)
         pick(0, 1, 0, SLOTS)
         cast_x(1, 0)
-        weave(0, 0, SLOTS)
-        quantize_x(0, 0, SLOTS)
+        weave(0, 0, SLOTS, "woven0")
         pick(1, 0, 0, SLOTS)
+        own_codes[0] = keep.tile([P, SLOTS], U32, name="own_codes0", tag="x_raw101", align_bytes=64)
+        quantize_x(0, 0, SLOTS)
         cast_x(1, 1)
-        pick(1, 1, 0, HALF_SLOTS)
-        weave(1, 0, HALF_SLOTS)
-        quantize_x(1, 0, HALF_SLOTS)
+        halves = ((0, HALF_SLOTS), (HALF_SLOTS, SLOTS))
+        for j0, j1 in halves:
+            pick(1, 1, j0, j1)
+        weave(1, 0, HALF_SLOTS, "woven1")
 
         w_codes, w_scales = {}, {}
 
@@ -164,7 +162,10 @@ def tile_moe_loc_lin_relu_kernel(tc, x_words, x_scales, xo, w, gate, offs, offs2
             grouped = keep.tile([P, PACK * N], BF16, name="w_grouped%d%d" % (e, s), align_bytes=64)
             src = w_raw[e, s][:].rearrange("p j (c i) -> p c j i", i=WALK)
             dst = grouped[:].rearrange("p (c i j) -> p c j i", i=WALK, j=PACK)
-            nc.scalar.activation(dst, src, COPY)
+            cut = W_SHARE.get((e, s), 0) // WALK
+            if cut:
+                nc.vector.tensor_copy(dst[:, :cut], src[:, :cut])
+            nc.scalar.activation(dst[:, cut:], src[:, cut:], COPY)
             w_codes[e, s] = keep.tile([P, N], U32, name="w_codes%d%d" % (e, s), align_bytes=64)
             if s == 0 and e > 0:
                 w_scales[e, s] = w_scales[e - 1, 1][SCALE_ROWS:P, :]
@@ -211,16 +212,18 @@ def tile_moe_loc_lin_relu_kernel(tc, x_words, x_scales, xo, w, gate, offs, offs2
             if e > 0:
                 multiply_own(e - 1, 1, 1)
                 scatter(e - 1, 0)
+            if e == 0:
+                quantize_x(1, 0, HALF_SLOTS)
             multiply_own(e, 0, 0)
             multiply_own(e, 1, 0)
             prepare_w(e, 1)
+            if e == 0:
+                weave(1, HALF_SLOTS, SLOTS, "w_raw01")
+            if e == 1:
+                quantize_x(1, HALF_SLOTS, SLOTS)
             if e > 0:
                 scatter(e - 1, 1)
             multiply_own(e, 0, 1)
-            if e == 0:
-                pick(1, 1, HALF_SLOTS, SLOTS)
-                weave(1, HALF_SLOTS, SLOTS)
-                quantize_x(1, HALF_SLOTS, SLOTS)
         multiply_own(last, 1, 1)
         for b in range(BLOCKS):
             scatter(last, b)
@@ -229,8 +232,8 @@ def tile_moe_loc_lin_relu_kernel(tc, x_words, x_scales, xo, w, gate, offs, offs2
         early = last * C
         for e in range(last):
             finish_far(e)
-        nc.sync.dma_start(out=out_rows[:, :, T:T + early], in_=far_out[:, :, :early])
+        nc.scalar.dma_start(out=out_rows[:, :, T:T + early], in_=far_out[:, :, :early])
         finish_far(last)
         nc.sync.dma_start(out=out_rows[:, 0, :T], in_=own_out[0][:])
-        nc.sync.dma_start(out=out_rows[:, :, T + early:], in_=far_out[:, :, early:])
+        nc.scalar.dma_start(out=out_rows[:, :, T + early:], in_=far_out[:, :, early:])
         nc.sync.dma_start(out=out_rows[:, 1, :T], in_=own_out[1][:])

@@ -27,7 +27,7 @@ SCALE_ROWS = 4
 PER_COLUMN = 16
 HALF_T = T // 2
 HALF_SLOTS = SLOTS // 2
-VECTOR_SHARE = {(0, 1, 1): 256}
+VECTOR_SHARE = {(0, 0): 320, (0, 1): 416, (1, 0): 480, (1, 1): 576}
 W_SHARE = {}
 WALK = 2
 
@@ -63,9 +63,8 @@ def tile_moe_loc_lin_relu_kernel(tc, x_words, x_scales, xo, w, gate, offs, offs2
             return rows[:, 2 * u:2 * u + 2, :]
 
         def load_x(s, u):
-            for h in range(2):
-                x_raw[s, u, h] = keep.tile([P, 2, HALF_T], F32, name="x_raw%d%d%d" % (s, u, h), tag="x_raw%d%d%d" % (s, u, h), align_bytes=64)[:]
-                nc.sync.dma_start(out=x_raw[s, u, h], in_=x_rows(s, u)[:, :, h * HALF_T:(h + 1) * HALF_T])
+            x_raw[s, u] = keep.tile([P, 2, T], F32, name="x_raw%d%d" % (s, u), tag="x_raw%d%d" % (s, u), align_bytes=64)
+            nc.sync.dma_start(out=x_raw[s, u][:], in_=x_rows(s, u))
 
         w_raw = {}
 
@@ -112,22 +111,23 @@ def tile_moe_loc_lin_relu_kernel(tc, x_words, x_scales, xo, w, gate, offs, offs2
 
         def cast_x(s, u):
             pairs = keep.tile([P, 2 * T], BF16, name="pairs%d%d" % (s, u), align_bytes=64)
-            for h in range(2):
-                dst = pairs[:, 2 * h * HALF_T:2 * (h + 1) * HALF_T].rearrange("p (t d) -> p t d", d=2)
-                src = x_raw[s, u, h].rearrange("p d t -> p t d")
-                cut = VECTOR_SHARE.get((s, u, h), 0)
-                if cut:
-                    nc.vector.tensor_copy(dst[:, :cut], src[:, :cut])
-                if cut < HALF_T:
-                    nc.scalar.activation(dst[:, cut:], src[:, cut:], COPY)
+            dst = pairs[:].rearrange("p (t d) -> p t d", d=2)
+            src = x_raw[s, u][:].rearrange("p d t -> p t d")
+            cut = VECTOR_SHARE[s, u]
+            nc.vector.tensor_copy(dst[:, :cut], src[:, :cut])
+            nc.scalar.activation(dst[:, cut:], src[:, cut:], COPY)
             pair_planes[s, u] = pairs
 
         def pick(s, u, j0, j1):
             entries = own_list[:, j0 // PER_COLUMN:j1 // PER_COLUMN]
             nc.vector.tensor_copy(picked[s][:, u, j0:j1], pair_planes[s, u][:].bitcast(U32).indirect(entries))
 
-        def weave(s, j0, j1, tag):
+        def weave(s, j0, j1, tag, on_scalar=False):
             woven[s, j0] = keep.tile([P, PACK * (j1 - j0)], BF16, name="woven%d_%d" % (s, j0), tag=tag, align_bytes=64)
+            if on_scalar:
+                words = woven[s, j0][:].bitcast(U32).rearrange("p (j u) -> p j u", u=2)
+                nc.scalar.copy(words, picked[s][:].rearrange("p u j -> p j u")[:, j0:j1, :])
+                return
             words = woven[s, j0][:].bitcast(I32).rearrange("p (j u) -> p j u", u=2)
             nc.vector.tensor_copy(words, picked[s][:].bitcast(I32).rearrange("p u j -> p j u")[:, j0:j1, :])
 
@@ -146,9 +146,9 @@ def tile_moe_loc_lin_relu_kernel(tc, x_words, x_scales, xo, w, gate, offs, offs2
         cast_x(0, 1)
         pick(0, 1, 0, SLOTS)
         cast_x(1, 0)
-        weave(0, 0, SLOTS, "woven0")
+        weave(0, 0, SLOTS, "x_raw10", on_scalar=True)
         pick(1, 0, 0, SLOTS)
-        own_codes[0] = keep.tile([P, SLOTS], U32, name="own_codes0", tag="x_raw101", align_bytes=64)
+        own_codes[0] = keep.tile([P, SLOTS], U32, name="own_codes0", align_bytes=64)
         quantize_x(0, 0, SLOTS)
         cast_x(1, 1)
         halves = ((0, HALF_SLOTS), (HALF_SLOTS, SLOTS))

@@ -1,6 +1,7 @@
 from contextlib import ExitStack
 
 import concourse.mybir as mybir
+from concourse.masks import make_identity
 
 K, T, Q, E, C, N = 1024, 1024, 768, 4, 128, 256
 SLOTS = E * C
@@ -16,6 +17,7 @@ FP8X4 = mybir.dt.float8_e4m3fn_x4
 COPY = mybir.ActivationFunctionType.Copy
 RELU = mybir.ActivationFunctionType.Relu
 MULT = mybir.AluOpType.mult
+MAX = mybir.AluOpType.max
 
 P = 128
 PACK = 4
@@ -25,11 +27,8 @@ BLOCKS = N // P
 QUADRANTS = 4
 SCALE_ROWS = 4
 PER_COLUMN = 16
-HALF_T = T // 2
-HALF_SLOTS = SLOTS // 2
-VECTOR_SHARE = {(0, 0): 320, (0, 1): 416, (1, 0): 480, (1, 1): 576}
-W_SHARE = {}
-WALK = 2
+HALF = SLOTS // 2
+WALK = 4
 
 
 def tile_moe_loc_lin_relu_kernel(tc, x_words, x_scales, xo, w, gate, offs, offs2, out):
@@ -39,37 +38,39 @@ def tile_moe_loc_lin_relu_kernel(tc, x_words, x_scales, xo, w, gate, offs, offs2
         keep = ctx.enter_context(tc.tile_pool(name="keep", bufs=1))
         psum = ctx.enter_context(tc.psum_pool(name="psum", bufs=1))
 
+        def sb(shape, dtype, name, tag=None):
+            return keep.tile(shape, dtype, name=name, tag=tag or name, align_bytes=64)
+
         own_list = lists.tile([P, SLOTS // PER_COLUMN], U16, name="own_list")
         far_list = lists.tile([P, SLOTS // PER_COLUMN], U16, name="far_list")
 
-        far_words = [keep.tile([P, Q], I32, name="far_words%d" % s, align_bytes=64) for s in range(PASSES)]
-        far_bytes = keep.tile([P, Q], U8, name="far_bytes", align_bytes=64)
-        far_codes = [keep.tile([P, SLOTS], U32, name="far_codes%d" % s, align_bytes=64) for s in range(PASSES)]
-        far_scales = keep.tile([P, SLOTS], U8, name="far_scales", align_bytes=64)
-        own_out = [keep.tile([P, T], F32, name="own_out%d" % b, align_bytes=64) for b in range(BLOCKS)]
-        gate_sb = keep.tile([P, SLOTS], F32, name="gate_sb", align_bytes=64)
+        far_words = [sb([P, Q], I32, "far_words%d" % s) for s in range(PASSES)]
+        far_bytes = sb([P, Q], U8, "far_bytes")
+        far_codes = [sb([P, SLOTS], U32, "far_codes%d" % s) for s in range(PASSES)]
+        far_scales = sb([P, SLOTS], U8, "far_scales")
+        own_out = [sb([P, T], F32, "own_out%d" % b) for b in range(BLOCKS)]
+        gate_sb = sb([P, SLOTS], F32, "gate_sb")
 
         nc.gpsimd.memset(far_bytes[:].bitcast(I32), 0)
-        for b in range(BLOCKS):
-            nc.gpsimd.memset(own_out[b][:], 0.0)
+        nc.gpsimd.memset(own_out[0][:], 0.0)
+        nc.scalar.activation(own_out[1][:], own_out[0][:], COPY)
 
         def load_words(s):
             nc.sync.dma_start(out=far_words[s][:], in_=x_words[s].rearrange("p t d -> p (t d)").bitcast(I32))
 
-        x_raw = {}
+        x_row = {}
 
-        def x_rows(s, u):
+        def load_x(s, j0, j1):
             rows = xo[s * K_PASS:(s + 1) * K_PASS, :].rearrange("(p j) t -> p j t", j=PACK)
-            return rows[:, 2 * u:2 * u + 2, :]
-
-        def load_x(s, u):
-            x_raw[s, u] = keep.tile([P, 2, T], F32, name="x_raw%d%d" % (s, u), tag="x_raw%d%d" % (s, u), align_bytes=64)
-            nc.sync.dma_start(out=x_raw[s, u][:], in_=x_rows(s, u))
+            raw = sb([P, j1 - j0, T], F32, "x_raw%d%d" % (s, j0))
+            nc.sync.dma_start(out=raw[:], in_=rows[:, j0:j1, :])
+            for j in range(j0, j1):
+                x_row[s, j] = raw[:, j - j0, :]
 
         w_raw = {}
 
         def load_w(e, s):
-            w_raw[e, s] = keep.tile([P, PACK, N], F32, name="w_raw%d%d" % (e, s), tag="w_raw%d%d" % (e, s), align_bytes=64)
+            w_raw[e, s] = sb([P, PACK, N], F32, "w_raw%d%d" % (e, s))
             nc.sync.dma_start(out=w_raw[e, s][:], in_=w[e, s * K_PASS:(s + 1) * K_PASS, :].rearrange("(p j) n -> p j n", j=PACK))
 
         def load_scales():
@@ -80,160 +81,182 @@ def tile_moe_loc_lin_relu_kernel(tc, x_words, x_scales, xo, w, gate, offs, offs2
                     in_=scale_rows[:, SCALE_ROWS * q:SCALE_ROWS * (q + 1), :],
                 )
 
-        def load_gate(e0, e1):
-            nc.sync.dma_start(out=gate_sb[:, e0 * C:e1 * C], in_=gate[:, e0 * C:e1 * C])
+        gate_cols = sb([P, SLOTS // P], F32, "gate_cols")
+        identity = sb([P, P], F32, "identity")
+        make_identity(nc, identity[:])
 
         load_words(0)
         nc.sync.dma_start(far_list[:], offs2)
         load_words(1)
-        load_scales()
-        load_x(0, 0)
         nc.sync.dma_start(own_list[:], offs)
-        load_x(0, 1)
-        load_x(1, 0)
-        load_x(1, 1)
+        load_x(0, 0, 1)
+        load_scales()
+        load_x(0, 1, 2)
+        nc.sync.dma_start(out=gate_cols[:], in_=gate[0].rearrange("(p i) -> p i", p=P))
+        load_x(0, 2, 4)
+        for j in range(PACK):
+            load_x(1, j, j + 1)
         for e in range(E):
             for s in range(PASSES):
                 load_w(e, s)
-                if (e, s) == (1, 0):
-                    load_gate(0, E // 2)
-        load_gate(E // 2, E)
 
-        def gather_words(s):
+        gate_bank = psum.tile([P, SLOTS // P, P], F32, name="gate_bank")
+        for i in range(SLOTS // P):
+            nc.tensor.transpose(gate_bank[:, i, :], gate_cols[:, i:i + 1].to_broadcast([P, P]), identity[:])
+        nc.scalar.activation(gate_sb[:].rearrange("m (p i) -> m p i", p=P), gate_bank[:].rearrange("m i p -> m p i"), COPY)
+
+        for s in range(PASSES):
             nc.vector.tensor_copy(far_codes[s][:], far_words[s][:].bitcast(U32).indirect(far_list[:]))
+        nc.vector.tensor_copy(far_scales[:], far_bytes[:].indirect(far_list[:]))
 
-        picked = [keep.tile([P, 2, SLOTS], U32, name="picked%d" % s, align_bytes=64) for s in range(PASSES)]
-        own_codes = {1: keep.tile([P, SLOTS], U32, name="own_codes1", align_bytes=64)}
-        own_scales = [keep.tile([P, SLOTS], U8, name="own_scales%d" % s, align_bytes=64) for s in range(PASSES)]
-        woven = {}
+        picked = [sb([P, PACK, SLOTS], F32, "picked%d" % s) for s in range(PASSES)]
 
-        pair_planes = {}
+        def entries(j0, j1):
+            return own_list[:, j0 // PER_COLUMN:j1 // PER_COLUMN]
 
-        def cast_x(s, u):
-            pairs = keep.tile([P, 2 * T], BF16, name="pairs%d%d" % (s, u), align_bytes=64)
-            dst = pairs[:].rearrange("p (t d) -> p t d", d=2)
-            src = x_raw[s, u][:].rearrange("p d t -> p t d")
-            cut = VECTOR_SHARE[s, u]
-            nc.vector.tensor_copy(dst[:, :cut], src[:, :cut])
-            nc.scalar.activation(dst[:, cut:], src[:, cut:], COPY)
-            pair_planes[s, u] = pairs
+        def pick(s, j, c0, c1, on_vector=False):
+            window = x_row[s, j].indirect(entries(c0, c1))
+            if on_vector:
+                nc.vector.tensor_copy(picked[s][:, j, c0:c1], window)
+            else:
+                nc.scalar.activation(picked[s][:, j, c0:c1], window, COPY)
 
-        def pick(s, u, j0, j1):
-            entries = own_list[:, j0 // PER_COLUMN:j1 // PER_COLUMN]
-            nc.vector.tensor_copy(picked[s][:, u, j0:j1], pair_planes[s, u][:].bitcast(U32).indirect(entries))
-
-        def weave(s, j0, j1, tag, on_scalar=False):
-            woven[s, j0] = keep.tile([P, PACK * (j1 - j0)], BF16, name="woven%d_%d" % (s, j0), tag=tag, align_bytes=64)
+        def interleave(grouped, rows, j0, j1, on_scalar=False):
+            src = rows.rearrange("p j (c i) -> p c j i", i=WALK)[:, :, j0:j1, :]
+            dst = grouped.rearrange("p (c i j) -> p c j i", i=WALK, j=PACK)[:, :, j0:j1, :]
             if on_scalar:
-                words = woven[s, j0][:].bitcast(U32).rearrange("p (j u) -> p j u", u=2)
-                nc.scalar.copy(words, picked[s][:].rearrange("p u j -> p j u")[:, j0:j1, :])
-                return
-            words = woven[s, j0][:].bitcast(I32).rearrange("p (j u) -> p j u", u=2)
-            nc.vector.tensor_copy(words, picked[s][:].bitcast(I32).rearrange("p u j -> p j u")[:, j0:j1, :])
+                nc.scalar.activation(dst, src, COPY)
+            else:
+                nc.vector.tensor_copy(dst, src)
 
-        def quantize_x(s, j0, j1):
+        x_grouped = [sb([P, PACK * SLOTS], BF16, "x_grouped%d" % s) for s in range(PASSES)]
+        own = {}
+
+        def weave_x(s, j0, j1, c0, c1):
+            interleave(x_grouped[s][:, PACK * c0:PACK * c1], picked[s][:, :, c0:c1], j0, j1)
+
+        def quantize_x(s, c0, c1, tag=None):
+            codes = sb([P, c1 - c0], U32, "own_codes%d_%d" % (s, c0), tag=tag)
+            scales = sb([P, c1 - c0], U8, "own_scales%d_%d" % (s, c0))
+            nc.vector.quantize_mx(out=codes[:].bitcast(FP8X4), scales=scales[:], in_=x_grouped[s][:, PACK * c0:PACK * c1])
+            for e in range(c0 // C, c1 // C):
+                cols = slice(e * C - c0, (e + 1) * C - c0)
+                own[e, s] = (codes[:, cols], scales[:, cols])
+
+        far = {}
+        for e in range(E):
+            for s in range(PASSES):
+                far[e, s] = (far_codes[s][:, e * C:(e + 1) * C], far_scales[SCALE_ROWS * s:P, e * C:(e + 1) * C])
+
+        w_grouped, w_codes, w_scales = {}, {}, {}
+
+        def cast_w(e, s, n0=0, n1=N, on_scalar=False):
+            if (e, s) not in w_grouped:
+                w_grouped[e, s] = sb([P, PACK * N], BF16, "w_grouped%d%d" % (e, s))
+                w_codes[e, s] = sb([P, N], U32, "w_codes%d%d" % (e, s))
+                w_scales[e, s] = sb([P, N], U8, "w_scales%d%d" % (e, s))
+            interleave(w_grouped[e, s][:, PACK * n0:PACK * n1], w_raw[e, s][:, :, n0:n1], 0, PACK, on_scalar)
+
+        def quantize_w(e, s, n0=0, n1=N):
             nc.vector.quantize_mx(
-                out=own_codes[s][:, j0:j1].bitcast(FP8X4),
-                scales=own_scales[s][:, j0:j1],
-                in_=woven[s, j0][:],
+                out=w_codes[e, s][:, n0:n1].bitcast(FP8X4),
+                scales=w_scales[e, s][:, n0:n1],
+                in_=w_grouped[e, s][:, PACK * n0:PACK * n1],
             )
 
-        gather_words(0)
-        gather_words(1)
-        nc.vector.tensor_copy(far_scales[:], far_bytes[:].indirect(far_list[:]))
-        cast_x(0, 0)
-        pick(0, 0, 0, SLOTS)
-        cast_x(0, 1)
-        pick(0, 1, 0, SLOTS)
-        cast_x(1, 0)
-        weave(0, 0, SLOTS, "x_raw10", on_scalar=True)
-        pick(1, 0, 0, SLOTS)
-        own_codes[0] = keep.tile([P, SLOTS], U32, name="own_codes0", align_bytes=64)
-        quantize_x(0, 0, SLOTS)
-        cast_x(1, 1)
-        halves = ((0, HALF_SLOTS), (HALF_SLOTS, SLOTS))
-        for j0, j1 in halves:
-            pick(1, 1, j0, j1)
-        weave(1, 0, HALF_SLOTS, "woven1")
-
-        w_codes, w_scales = {}, {}
-
-        def prepare_w(e, s):
-            grouped = keep.tile([P, PACK * N], BF16, name="w_grouped%d%d" % (e, s), align_bytes=64)
-            src = w_raw[e, s][:].rearrange("p j (c i) -> p c j i", i=WALK)
-            dst = grouped[:].rearrange("p (c i j) -> p c j i", i=WALK, j=PACK)
-            cut = W_SHARE.get((e, s), 0) // WALK
-            if cut:
-                nc.vector.tensor_copy(dst[:, :cut], src[:, :cut])
-            nc.scalar.activation(dst[:, cut:], src[:, cut:], COPY)
-            w_codes[e, s] = keep.tile([P, N], U32, name="w_codes%d%d" % (e, s), align_bytes=64)
-            if s == 0 and e > 0:
-                w_scales[e, s] = w_scales[e - 1, 1][SCALE_ROWS:P, :]
-            else:
-                w_scales[e, s] = keep.tile([P, N], U8, name="w_scales%d%d" % (e, s), align_bytes=64)[:]
-            nc.vector.quantize_mx(out=w_codes[e, s][:].bitcast(FP8X4), scales=w_scales[e, s], in_=grouped[:])
-
-        def multiply(acc, e, b, s, codes, scales):
+        def multiply(acc, e, s, b, tokens, start, stop):
             cols = slice(b * P, (b + 1) * P)
             nc.tensor.matmul_mx(
                 out=acc,
                 lhsT=w_codes[e, s][:, cols].bitcast(FP8X4),
                 lhsT_scale=w_scales[e, s][:, cols],
-                rhs=codes[:, e * C:(e + 1) * C].bitcast(FP8X4),
-                rhs_scale=scales[:, e * C:(e + 1) * C],
-                start=(s == 0),
-                stop=(s == PASSES - 1),
+                rhs=tokens[e, s][0].bitcast(FP8X4),
+                rhs_scale=tokens[e, s][1],
+                start=start,
+                stop=stop,
             )
 
-        own_banks = {}
-
-        def multiply_own(e, b, s):
-            if s == 0:
-                own_banks[e, b] = psum.tile([P, C], F32, name="own_bank%d" % b, bufs=2)
-            multiply(own_banks[e, b][:], e, b, s, own_codes[s], own_scales[s])
-
-        def scatter(e, b):
-            y = keep.tile([P, C], F32, name="y%d%d" % (e, b), align_bytes=64)
-            nc.scalar.activation(y[:], own_banks[e, b][:], RELU)
-            entries = own_list[:, e * C // PER_COLUMN:(e + 1) * C // PER_COLUMN]
-            nc.vector.tensor_tensor(own_out[b][:].indirect(entries), y[:], gate_sb[:, e * C:(e + 1) * C], MULT)
-
-        def finish_far(e):
-            bank = psum.tile([P, BLOCKS, C], F32, name="far_bank%d" % e)
+        def multiply_bank(bank, e, s, tokens):
             for b in range(BLOCKS):
-                for s in range(PASSES):
-                    multiply(bank[:, b, :], e, b, s, far_codes[s], far_scales[SCALE_ROWS * s:P, :])
-            nc.scalar.activation(far_out[:, :, e * C:(e + 1) * C], bank[:], RELU)
+                multiply(bank[:, b, :], e, s, b, tokens, s == 0 and b == 0, s == PASSES - 1 and b == BLOCKS - 1)
+
+        far_early = sb([P, BLOCKS, HALF], F32, "far_early")
+
+        def finish_far(e, dst, on_vector=False):
+            bank = psum.tile([P, BLOCKS, C], F32, name="far_bank", bufs=2)
+            for s in range(PASSES):
+                multiply_bank(bank, e, s, far)
+            if on_vector:
+                nc.vector.tensor_scalar_max(dst, bank[:], 0.0)
+            else:
+                nc.scalar.activation(dst, bank[:], RELU)
+
+        def window(e, b):
+            return own_out[b][:].indirect(entries(e * C, (e + 1) * C))
+
+        pick(0, 0, 0, SLOTS)
+        pick(0, 1, 0, SLOTS)
+        weave_x(0, 0, 2, 0, SLOTS)
+        pick(0, 2, 0, SLOTS)
+        pick(0, 3, 0, SLOTS, on_vector=True)
+        weave_x(0, 2, 4, 0, SLOTS)
+        quantize_x(0, 0, SLOTS)
+        pick(1, 0, 0, SLOTS)
+        pick(1, 1, 0, SLOTS)
+        weave_x(1, 0, 2, 0, SLOTS)
+        pick(1, 2, 0, SLOTS)
+        pick(1, 3, 0, C, on_vector=True)
+        pick(1, 3, C, HALF)
+        pick(1, 3, HALF, SLOTS)
+        weave_x(1, 2, 4, 0, C)
+        weave_x(1, 2, 4, C, HALF)
+        quantize_x(1, 0, C)
+        quantize_x(1, C, HALF)
+        weave_x(1, 2, 4, HALF, SLOTS)
+        quantize_x(1, HALF, SLOTS)
 
         last = E - 1
         out_rows = out.rearrange("(b p) c -> p b c", p=P)
-        for e in range(E):
-            prepare_w(e, 0)
-            if e > 0:
-                multiply_own(e - 1, 1, 1)
-                scatter(e - 1, 0)
-            if e == 0:
-                quantize_x(1, 0, HALF_SLOTS)
-            multiply_own(e, 0, 0)
-            multiply_own(e, 1, 0)
-            prepare_w(e, 1)
-            if e == 0:
-                weave(1, HALF_SLOTS, SLOTS, "w_raw01")
-            if e == 1:
-                quantize_x(1, HALF_SLOTS, SLOTS)
-            if e > 0:
-                scatter(e - 1, 1)
-            multiply_own(e, 0, 1)
-        multiply_own(last, 1, 1)
-        for b in range(BLOCKS):
-            scatter(last, b)
-
-        far_out = keep.tile([P, BLOCKS, SLOTS], F32, name="far_out", tag="w_raw%d%d" % (last, PASSES - 1), align_bytes=64)
-        early = last * C
+        ys = []
         for e in range(last):
-            finish_far(e)
-        nc.scalar.dma_start(out=out_rows[:, :, T:T + early], in_=far_out[:, :, :early])
-        finish_far(last)
-        nc.sync.dma_start(out=out_rows[:, 0, :T], in_=own_out[0][:])
-        nc.scalar.dma_start(out=out_rows[:, :, T + early:], in_=far_out[:, :, early:])
+            own_bank = psum.tile([P, BLOCKS, C], F32, name="own_bank", bufs=2)
+            cast_w(e, 0, on_scalar=(e < 2))
+            if e == 0:
+                cast_w(e, 1, 0, P)
+                cast_w(e, 1, P, N, on_scalar=True)
+            else:
+                cast_w(e, 1)
+            for s in range(PASSES):
+                quantize_w(e, s)
+                multiply_bank(own_bank, e, s, own)
+            y = sb([P, BLOCKS, C], F32, "y%d" % e)
+            ys.append(y)
+            g = gate_sb[:, e * C:(e + 1) * C].unsqueeze(1).to_broadcast([P, BLOCKS, C])
+            nc.vector.scalar_tensor_tensor(y[:], own_bank[:], 0.0, g, MAX, MULT)
+            for b in range(BLOCKS):
+                nc.scalar.activation(window(e, b), y[:, b, :], COPY)
+            if e < 2:
+                finish_far(e, far_early[:, :, e * C:(e + 1) * C])
+        nc.sync.dma_start(out=out_rows[:, :, T:T + HALF], in_=far_early[:])
+
+        cast_w(last, 0)
+        cast_w(last, 1, 0, P)
+        cast_w(last, 1, P, N)
+        quantize_w(last, 0)
+        banks = [psum.tile([P, C], F32, name="last_bank%d" % b) for b in range(BLOCKS)]
+        for b in range(BLOCKS):
+            multiply(banks[b][:], last, 0, b, own, True, False)
+        for b in range(BLOCKS):
+            quantize_w(last, 1, b * P, (b + 1) * P)
+            multiply(banks[b][:], last, 1, b, own, False, True)
+        far_late = sb([P, BLOCKS, HALF], F32, "far_late", tag="w_grouped31")
+        finish_far(2, far_late[:, :, :C], on_vector=True)
+        y = [sb([P, C], F32, "y_last%d" % b) for b in range(BLOCKS)]
+        for b in range(BLOCKS):
+            nc.vector.scalar_tensor_tensor(y[b][:], banks[b][:], 0.0, gate_sb[:, last * C:], MAX, MULT)
+        nc.scalar.activation(window(last, 0), y[0][:], COPY)
+        finish_far(last, far_late[:, :, C:], on_vector=True)
+        nc.vector.tensor_copy(window(last, 1), y[1][:])
+        nc.sync.dma_start(out=out_rows[:, :, T + HALF:], in_=far_late[:])
+        nc.scalar.dma_start(out=out_rows[:, 0, :T], in_=own_out[0][:])
         nc.sync.dma_start(out=out_rows[:, 1, :T], in_=own_out[1][:])

@@ -88,14 +88,14 @@ def tile_moe_loc_lin_relu_kernel(tc, x_words, x_scales, xo, w, gate, offs, offs2
         load_words(0)
         nc.sync.dma_start(far_list[:], offs2)
         load_words(1)
-        nc.sync.dma_start(own_list[:], offs)
-        load_x(0, 0, 1)
+        load_x(0, 0, 2)
         load_scales()
-        load_x(0, 1, 2)
-        nc.sync.dma_start(out=gate_cols[:], in_=gate[0].rearrange("(p i) -> p i", p=P))
+        nc.sync.dma_start(own_list[:], offs)
         load_x(0, 2, 4)
-        for j in range(PACK):
-            load_x(1, j, j + 1)
+        nc.sync.dma_start(out=gate_cols[:], in_=gate[0].rearrange("(p i) -> p i", p=P))
+        load_x(1, 0, 2)
+        load_x(1, 2, 3)
+        load_x(1, 3, 4)
         for e in range(E):
             for s in range(PASSES):
                 load_w(e, s)
@@ -196,16 +196,15 @@ def tile_moe_loc_lin_relu_kernel(tc, x_words, x_scales, xo, w, gate, offs, offs2
 
         pick(0, 0, 0, SLOTS)
         pick(0, 1, 0, SLOTS)
-        weave_x(0, 0, 2, 0, SLOTS)
         pick(0, 2, 0, SLOTS)
         pick(0, 3, 0, SLOTS, on_vector=True)
-        weave_x(0, 2, 4, 0, SLOTS)
+        weave_x(0, 0, 4, 0, SLOTS)
         quantize_x(0, 0, SLOTS)
         pick(1, 0, 0, SLOTS)
-        pick(1, 1, 0, SLOTS)
+        pick(1, 1, 0, SLOTS, on_vector=True)
         weave_x(1, 0, 2, 0, SLOTS)
         pick(1, 2, 0, SLOTS)
-        pick(1, 3, 0, C, on_vector=True)
+        pick(1, 3, 0, C)
         pick(1, 3, C, HALF)
         pick(1, 3, HALF, SLOTS)
         weave_x(1, 2, 4, 0, C)
@@ -213,7 +212,6 @@ def tile_moe_loc_lin_relu_kernel(tc, x_words, x_scales, xo, w, gate, offs, offs2
         quantize_x(1, 0, C)
         quantize_x(1, C, HALF)
         weave_x(1, 2, 4, HALF, SLOTS)
-        quantize_x(1, HALF, SLOTS)
 
         last = E - 1
         out_rows = out.rearrange("(b p) c -> p b c", p=P)
@@ -229,6 +227,8 @@ def tile_moe_loc_lin_relu_kernel(tc, x_words, x_scales, xo, w, gate, offs, offs2
             for s in range(PASSES):
                 quantize_w(e, s)
                 multiply_bank(own_bank, e, s, own)
+            if e == 0:
+                quantize_x(1, HALF, SLOTS, tag="w_raw01")
             y = sb([P, BLOCKS, C], F32, "y%d" % e)
             ys.append(y)
             g = gate_sb[:, e * C:(e + 1) * C].unsqueeze(1).to_broadcast([P, BLOCKS, C])
@@ -252,10 +252,10 @@ def tile_moe_loc_lin_relu_kernel(tc, x_words, x_scales, xo, w, gate, offs, offs2
         far_late = sb([P, BLOCKS, HALF], F32, "far_late", tag="w_grouped31")
         finish_far(2, far_late[:, :, :C], on_vector=True)
         y = [sb([P, C], F32, "y_last%d" % b) for b in range(BLOCKS)]
-        for b in range(BLOCKS):
-            nc.vector.scalar_tensor_tensor(y[b][:], banks[b][:], 0.0, gate_sb[:, last * C:], MAX, MULT)
+        nc.vector.scalar_tensor_tensor(y[0][:], banks[0][:], 0.0, gate_sb[:, last * C:], MAX, MULT)
         nc.scalar.activation(window(last, 0), y[0][:], COPY)
         finish_far(last, far_late[:, :, C:], on_vector=True)
+        nc.vector.scalar_tensor_tensor(y[1][:], banks[1][:], 0.0, gate_sb[:, last * C:], MAX, MULT)
         nc.vector.tensor_copy(window(last, 1), y[1][:])
         nc.sync.dma_start(out=out_rows[:, :, T + HALF:], in_=far_late[:])
         nc.scalar.dma_start(out=out_rows[:, 0, :T], in_=own_out[0][:])

@@ -81,29 +81,35 @@ def tile_moe_loc_lin_relu_kernel(tc, x_words, x_scales, xo, w, gate, offs, offs2
                     in_=scale_rows[:, SCALE_ROWS * q:SCALE_ROWS * (q + 1), :],
                 )
 
-        gate_cols = sb([P, SLOTS // P], F32, "gate_cols")
+        gate_rows = sb([P, C], F32, "gate_rows")
+        gate_cols = sb([P, E], F32, "gate_cols")
+        nc.vector.memset(gate_rows[:], 0.0)
         identity = sb([P, P], F32, "identity")
         make_identity(nc, identity[:])
 
         load_words(0)
         nc.sync.dma_start(far_list[:], offs2)
-        load_words(1)
-        load_x(0, 0, 2)
-        load_scales()
         nc.sync.dma_start(own_list[:], offs)
-        load_x(0, 2, 4)
-        nc.sync.dma_start(out=gate_cols[:], in_=gate[0].rearrange("(p i) -> p i", p=P))
-        load_x(1, 0, 2)
-        load_x(1, 2, 3)
-        load_x(1, 3, 4)
+        load_words(1)
+        nc.sync.dma_start(out=gate_rows[:E, :], in_=gate[0].rearrange("(e c) -> e c", e=E))
+        load_x(0, 0, 1)
+        load_x(0, 1, 2)
+        load_scales()
+        load_x(0, 2, 3)
+        load_x(0, 3, 4)
+        for j in range(PACK):
+            load_x(1, j, j + 1)
         for e in range(E):
             for s in range(PASSES):
                 load_w(e, s)
 
-        gate_bank = psum.tile([P, SLOTS // P, P], F32, name="gate_bank")
-        for i in range(SLOTS // P):
-            nc.tensor.transpose(gate_bank[:, i, :], gate_cols[:, i:i + 1].to_broadcast([P, P]), identity[:])
-        nc.scalar.activation(gate_sb[:].rearrange("m (p i) -> m p i", p=P), gate_bank[:].rearrange("m i p -> m p i"), COPY)
+        turned = psum.tile([P, P], F32, name="turned", tag="gate_bank")
+        nc.tensor.transpose(turned[:], gate_rows[:], identity[:])
+        nc.vector.tensor_copy(gate_cols[:], turned[:, :E])
+        gate_bank = psum.tile([P, SLOTS], F32, name="gate_bank", tag="gate_bank")
+        for e in range(E):
+            nc.tensor.transpose(gate_bank[:, e * C:(e + 1) * C], gate_cols[:, e:e + 1].to_broadcast([P, P]), identity[:])
+        nc.vector.tensor_copy(gate_sb[:], gate_bank[:])
 
         for s in range(PASSES):
             nc.vector.tensor_copy(far_codes[s][:], far_words[s][:].bitcast(U32).indirect(far_list[:]))
@@ -201,17 +207,14 @@ def tile_moe_loc_lin_relu_kernel(tc, x_words, x_scales, xo, w, gate, offs, offs2
         weave_x(0, 0, 4, 0, SLOTS)
         quantize_x(0, 0, SLOTS)
         pick(1, 0, 0, SLOTS)
-        pick(1, 1, 0, SLOTS, on_vector=True)
+        pick(1, 1, 0, SLOTS)
         weave_x(1, 0, 2, 0, SLOTS)
         pick(1, 2, 0, SLOTS)
-        pick(1, 3, 0, C)
-        pick(1, 3, C, HALF)
+        pick(1, 3, 0, HALF, on_vector=True)
         pick(1, 3, HALF, SLOTS)
-        weave_x(1, 2, 4, 0, C)
-        weave_x(1, 2, 4, C, HALF)
-        quantize_x(1, 0, C)
-        quantize_x(1, C, HALF)
+        weave_x(1, 2, 4, 0, HALF)
         weave_x(1, 2, 4, HALF, SLOTS)
+        quantize_x(1, 0, HALF)
 
         last = E - 1
         out_rows = out.rearrange("(b p) c -> p b c", p=P)

@@ -189,7 +189,7 @@ def tile_moe_loc_lin_relu_kernel(tc, x_words, x_scales, xo, w, gate, offs, offs2
         far_early = sb([P, BLOCKS, HALF], F32, "far_early")
 
         def finish_far(e, dst, on_vector=False):
-            bank = psum.tile([P, BLOCKS, C], F32, name="far_bank", bufs=2)
+            bank = psum.tile([P, BLOCKS, C], F32, name="far_bank%d" % e, tag="bank%d" % e)
             for s in range(PASSES):
                 multiply_bank(bank, e, s, far)
             if on_vector:
@@ -208,23 +208,23 @@ def tile_moe_loc_lin_relu_kernel(tc, x_words, x_scales, xo, w, gate, offs, offs2
         quantize_x(0, 0, SLOTS)
         pick(1, 0, 0, SLOTS)
         pick(1, 1, 0, SLOTS)
-        weave_x(1, 0, 2, 0, SLOTS)
+        weave_x(1, 0, 2, 0, HALF)
         pick(1, 2, 0, SLOTS)
         pick(1, 3, 0, HALF, on_vector=True)
         pick(1, 3, HALF, SLOTS)
         weave_x(1, 2, 4, 0, HALF)
-        weave_x(1, 2, 4, HALF, SLOTS)
+        weave_x(1, 0, 4, HALF, SLOTS)
         quantize_x(1, 0, HALF)
 
         last = E - 1
         out_rows = out.rearrange("(b p) c -> p b c", p=P)
         ys = []
         for e in range(last):
-            own_bank = psum.tile([P, BLOCKS, C], F32, name="own_bank", bufs=2)
+            own_bank = psum.tile([P, BLOCKS, C], F32, name="own_bank%d" % e, tag="bank%d" % e)
             cast_w(e, 0, on_scalar=(e < 2))
             if e == 0:
-                cast_w(e, 1, 0, P)
-                cast_w(e, 1, P, N, on_scalar=True)
+                cast_w(e, 1, 0, 96)
+                cast_w(e, 1, 96, N, on_scalar=True)
             else:
                 cast_w(e, 1)
             for s in range(PASSES):

@@ -49,7 +49,6 @@ def tile_moe_loc_lin_relu_kernel(tc, x_words, x_scales, xo, w, gate, offs, offs2
         far_codes = [sb([P, SLOTS], U32, "far_codes%d" % s) for s in range(PASSES)]
         far_scales = sb([P, SLOTS], U8, "far_scales")
         own_out = [sb([P, T], F32, "own_out%d" % b) for b in range(BLOCKS)]
-        gate_sb = sb([P, SLOTS], F32, "gate_sb")
 
         nc.gpsimd.memset(far_bytes[:].bitcast(I32), 0)
         nc.gpsimd.memset(own_out[0][:], 0.0)
@@ -109,7 +108,6 @@ def tile_moe_loc_lin_relu_kernel(tc, x_words, x_scales, xo, w, gate, offs, offs2
         gate_bank = psum.tile([P, SLOTS], F32, name="gate_bank", tag="gate_bank")
         for e in range(E):
             nc.tensor.transpose(gate_bank[:, e * C:(e + 1) * C], gate_cols[:, e:e + 1].to_broadcast([P, P]), identity[:])
-        nc.vector.tensor_copy(gate_sb[:], gate_bank[:])
 
         for s in range(PASSES):
             nc.vector.tensor_copy(far_codes[s][:], far_words[s][:].bitcast(U32).indirect(far_list[:]))
@@ -188,6 +186,13 @@ def tile_moe_loc_lin_relu_kernel(tc, x_words, x_scales, xo, w, gate, offs, offs2
 
         far_early = sb([P, BLOCKS, HALF], F32, "far_early")
 
+        def finish_early_far():
+            bank = psum.tile([P, BLOCKS, HALF], F32, name="far_bank01", tag="bank1")
+            steps = [(e, s, b) for e in range(2) for s in range(PASSES) for b in range(BLOCKS)]
+            for e, s, b in steps:
+                multiply(bank[:, b, e * C:(e + 1) * C], e, s, b, far, (e, s, b) == steps[0], (e, s, b) == steps[-1])
+            nc.scalar.activation(far_early[:], bank[:], RELU)
+
         def finish_far(e, dst, on_vector=False):
             bank = psum.tile([P, BLOCKS, C], F32, name="far_bank%d" % e, tag="bank%d" % e)
             for s in range(PASSES):
@@ -205,7 +210,7 @@ def tile_moe_loc_lin_relu_kernel(tc, x_words, x_scales, xo, w, gate, offs, offs2
         pick(0, 2, 0, SLOTS)
         pick(0, 3, 0, SLOTS, on_vector=True)
         weave_x(0, 0, 4, 0, SLOTS)
-        quantize_x(0, 0, SLOTS)
+        quantize_x(0, 0, HALF)
         pick(1, 0, 0, SLOTS)
         pick(1, 1, 0, SLOTS)
         weave_x(1, 0, 2, 0, HALF)
@@ -221,25 +226,33 @@ def tile_moe_loc_lin_relu_kernel(tc, x_words, x_scales, xo, w, gate, offs, offs2
         ys = []
         for e in range(last):
             own_bank = psum.tile([P, BLOCKS, C], F32, name="own_bank%d" % e, tag="bank%d" % e)
-            cast_w(e, 0, on_scalar=(e < 2))
+            if e == 2:
+                cast_w(e, 0, 0, 192)
+                cast_w(e, 0, 192, N, on_scalar=True)
+            else:
+                cast_w(e, 0, on_scalar=True)
             if e == 0:
                 cast_w(e, 1, 0, 96)
                 cast_w(e, 1, 96, N, on_scalar=True)
             else:
                 cast_w(e, 1)
+            if e == 0:
+                gate_sb = sb([P, SLOTS], F32, "gate_sb", tag="w_raw00")
+                nc.scalar.activation(gate_sb[:], gate_bank[:], COPY)
             for s in range(PASSES):
                 quantize_w(e, s)
                 multiply_bank(own_bank, e, s, own)
             if e == 0:
                 quantize_x(1, HALF, SLOTS, tag="w_raw01")
+                quantize_x(0, HALF, SLOTS, tag="w_grouped01")
             y = sb([P, BLOCKS, C], F32, "y%d" % e)
             ys.append(y)
             g = gate_sb[:, e * C:(e + 1) * C].unsqueeze(1).to_broadcast([P, BLOCKS, C])
             nc.vector.scalar_tensor_tensor(y[:], own_bank[:], 0.0, g, MAX, MULT)
             for b in range(BLOCKS):
                 nc.scalar.activation(window(e, b), y[:, b, :], COPY)
-            if e < 2:
-                finish_far(e, far_early[:, :, e * C:(e + 1) * C])
+            if e == 1:
+                finish_early_far()
         nc.sync.dma_start(out=out_rows[:, :, T:T + HALF], in_=far_early[:])
 
         cast_w(last, 0)

@@ -28,6 +28,7 @@ QUADRANTS = 4
 SCALE_ROWS = 4
 PER_COLUMN = 16
 HALF = SLOTS // 2
+VECTOR_COLUMNS = ((0, 96), (0, 256), (192, 256))
 WALK = 4
 
 
@@ -104,7 +105,7 @@ def tile_moe_loc_lin_relu_kernel(tc, x_words, x_scales, xo, w, gate, offs, offs2
 
         turned = psum.tile([P, P], F32, name="turned", tag="gate_bank")
         nc.tensor.transpose(turned[:], gate_rows[:], identity[:])
-        nc.vector.tensor_copy(gate_cols[:], turned[:, :E])
+        nc.scalar.activation(gate_cols[:], turned[:, :E], COPY)
         gate_bank = psum.tile([P, SLOTS], F32, name="gate_bank", tag="gate_bank")
         for e in range(E):
             nc.tensor.transpose(gate_bank[:, e * C:(e + 1) * C], gate_cols[:, e:e + 1].to_broadcast([P, P]), identity[:])
@@ -136,8 +137,8 @@ def tile_moe_loc_lin_relu_kernel(tc, x_words, x_scales, xo, w, gate, offs, offs2
         x_grouped = [sb([P, PACK * SLOTS], BF16, "x_grouped%d" % s) for s in range(PASSES)]
         own = {}
 
-        def weave_x(s, j0, j1, c0, c1):
-            interleave(x_grouped[s][:, PACK * c0:PACK * c1], picked[s][:, :, c0:c1], j0, j1)
+        def weave_x(s, j0, j1, c0, c1, on_scalar=False):
+            interleave(x_grouped[s][:, PACK * c0:PACK * c1], picked[s][:, :, c0:c1], j0, j1, on_scalar)
 
         def quantize_x(s, c0, c1, tag=None):
             codes = sb([P, c1 - c0], U32, "own_codes%d_%d" % (s, c0), tag=tag)
@@ -205,14 +206,20 @@ def tile_moe_loc_lin_relu_kernel(tc, x_words, x_scales, xo, w, gate, offs, offs2
         def window(e, b):
             return own_out[b][:].indirect(entries(e * C, (e + 1) * C))
 
-        pick(0, 0, 0, SLOTS)
+        def share(s, j):
+            pick(s, j, 0, HALF)
+            pick(s, j, HALF, SLOTS, on_vector=True)
+
+        share(0, 0)
         pick(0, 1, 0, SLOTS)
-        pick(0, 2, 0, SLOTS)
-        pick(0, 3, 0, SLOTS, on_vector=True)
+        share(0, 2)
+        share(0, 3)
+        gate_sb = sb([P, SLOTS], F32, "gate_sb", tag="x_raw03")
+        nc.scalar.activation(gate_sb[:], gate_bank[:], COPY)
         weave_x(0, 0, 4, 0, SLOTS)
+        share(1, 0)
         quantize_x(0, 0, HALF)
-        pick(1, 0, 0, SLOTS)
-        pick(1, 1, 0, SLOTS)
+        share(1, 1)
         weave_x(1, 0, 2, 0, HALF)
         pick(1, 2, 0, SLOTS)
         pick(1, 3, 0, HALF, on_vector=True)
@@ -226,19 +233,12 @@ def tile_moe_loc_lin_relu_kernel(tc, x_words, x_scales, xo, w, gate, offs, offs2
         ys = []
         for e in range(last):
             own_bank = psum.tile([P, BLOCKS, C], F32, name="own_bank%d" % e, tag="bank%d" % e)
-            if e == 2:
-                cast_w(e, 0, 0, 192)
-                cast_w(e, 0, 192, N, on_scalar=True)
-            else:
-                cast_w(e, 0, on_scalar=True)
-            if e == 0:
-                cast_w(e, 1, 0, 96)
-                cast_w(e, 1, 96, N, on_scalar=True)
-            else:
-                cast_w(e, 1)
-            if e == 0:
-                gate_sb = sb([P, SLOTS], F32, "gate_sb", tag="w_raw00")
-                nc.scalar.activation(gate_sb[:], gate_bank[:], COPY)
+            for s in range(PASSES):
+                cut = VECTOR_COLUMNS[e][s]
+                if cut > 0:
+                    cast_w(e, s, 0, cut)
+                if cut < N:
+                    cast_w(e, s, cut, N, on_scalar=True)
             for s in range(PASSES):
                 quantize_w(e, s)
                 multiply_bank(own_bank, e, s, own)
@@ -256,9 +256,9 @@ def tile_moe_loc_lin_relu_kernel(tc, x_words, x_scales, xo, w, gate, offs, offs2
         nc.sync.dma_start(out=out_rows[:, :, T:T + HALF], in_=far_early[:])
 
         cast_w(last, 0)
+        quantize_w(last, 0)
         cast_w(last, 1, 0, P)
         cast_w(last, 1, P, N)
-        quantize_w(last, 0)
         banks = [psum.tile([P, C], F32, name="last_bank%d" % b) for b in range(BLOCKS)]
         for b in range(BLOCKS):
             multiply(banks[b][:], last, 0, b, own, True, False)

@@ -28,7 +28,7 @@ QUADRANTS = 4
 SCALE_ROWS = 4
 PER_COLUMN = 16
 HALF = SLOTS // 2
-VECTOR_COLUMNS = ((0, 96), (0, 256), (192, 256))
+VECTOR_COLUMNS = ((0, 96), (0, 256), (256, 256))
 WALK = 4
 
 

@@ -28,7 +28,7 @@ QUADRANTS = 4
 SCALE_ROWS = 4
 PER_COLUMN = 16
 HALF = SLOTS // 2
-VECTOR_COLUMNS = ((0, 96), (0, 256), (256, 256))
+VECTOR_COLUMNS = ((0, 176), (0, 256), (256, 256))
 WALK = 4
 
 
@@ -187,13 +187,6 @@ def tile_moe_loc_lin_relu_kernel(tc, x_words, x_scales, xo, w, gate, offs, offs2
 
         far_early = sb([P, BLOCKS, HALF], F32, "far_early")
 
-        def finish_early_far():
-            bank = psum.tile([P, BLOCKS, HALF], F32, name="far_bank01", tag="bank1")
-            steps = [(e, s, b) for e in range(2) for s in range(PASSES) for b in range(BLOCKS)]
-            for e, s, b in steps:
-                multiply(bank[:, b, e * C:(e + 1) * C], e, s, b, far, (e, s, b) == steps[0], (e, s, b) == steps[-1])
-            nc.scalar.activation(far_early[:], bank[:], RELU)
-
         def finish_far(e, dst, on_vector=False):
             bank = psum.tile([P, BLOCKS, C], F32, name="far_bank%d" % e, tag="bank%d" % e)
             for s in range(PASSES):
@@ -222,7 +215,8 @@ def tile_moe_loc_lin_relu_kernel(tc, x_words, x_scales, xo, w, gate, offs, offs2
         share(1, 1)
         weave_x(1, 0, 2, 0, HALF)
         pick(1, 2, 0, SLOTS)
-        pick(1, 3, 0, HALF, on_vector=True)
+        pick(1, 3, 0, C, on_vector=True)
+        pick(1, 3, C, HALF)
         pick(1, 3, HALF, SLOTS)
         weave_x(1, 2, 4, 0, HALF)
         weave_x(1, 0, 4, HALF, SLOTS)
@@ -251,8 +245,8 @@ def tile_moe_loc_lin_relu_kernel(tc, x_words, x_scales, xo, w, gate, offs, offs2
             nc.vector.scalar_tensor_tensor(y[:], own_bank[:], 0.0, g, MAX, MULT)
             for b in range(BLOCKS):
                 nc.scalar.activation(window(e, b), y[:, b, :], COPY)
-            if e == 1:
-                finish_early_far()
+            if e < 2:
+                finish_far(e, far_early[:, :, e * C:(e + 1) * C])
         nc.sync.dma_start(out=out_rows[:, :, T:T + HALF], in_=far_early[:])
 
         cast_w(last, 0)

@@ -51,7 +51,6 @@ def tile_moe_loc_lin_relu_kernel(tc, x_words, x_scales, xo, w, gate, offs, offs2
         far_scales = sb([P, SLOTS], U8, "far_scales")
         own_out = [sb([P, T], F32, "own_out%d" % b) for b in range(BLOCKS)]
 
-        nc.gpsimd.memset(far_bytes[:].bitcast(I32), 0)
         nc.gpsimd.memset(own_out[0][:], 0.0)
         nc.scalar.activation(own_out[1][:], own_out[0][:], COPY)
 
@@ -76,7 +75,7 @@ def tile_moe_loc_lin_relu_kernel(tc, x_words, x_scales, xo, w, gate, offs, offs2
         def load_scales():
             scale_rows = x_scales.bitcast(I32)
             for q in range(QUADRANTS):
-                nc.sync.dma_start(
+                nc.scalar.dma_start(
                     out=far_bytes[32 * q:32 * q + SCALE_ROWS * PASSES, :].bitcast(I32),
                     in_=scale_rows[:, SCALE_ROWS * q:SCALE_ROWS * (q + 1), :],
                 )
@@ -86,6 +85,7 @@ def tile_moe_loc_lin_relu_kernel(tc, x_words, x_scales, xo, w, gate, offs, offs2
         nc.vector.memset(gate_rows[:], 0.0)
         identity = sb([P, P], F32, "identity")
         make_identity(nc, identity[:])
+        nc.gpsimd.memset(far_bytes[:].bitcast(I32), 0)
 
         load_words(0)
         nc.sync.dma_start(far_list[:], offs2)

@@ -18,6 +18,7 @@ COPY = mybir.ActivationFunctionType.Copy
 RELU = mybir.ActivationFunctionType.Relu
 MULT = mybir.AluOpType.mult
 MAX = mybir.AluOpType.max
+ADD = mybir.AluOpType.add
 
 P = 128
 PACK = 4
@@ -114,7 +115,14 @@ def tile_moe_loc_lin_relu_kernel(tc, x_words, x_scales, xo, w, gate, offs, offs2
             nc.vector.tensor_copy(far_codes[s][:], far_words[s][:].bitcast(U32).indirect(far_list[:]))
         nc.vector.tensor_copy(far_scales[:], far_bytes[:].indirect(far_list[:]))
 
-        picked = [sb([P, PACK, SLOTS], F32, "picked%d" % s) for s in range(PASSES)]
+        picked_halves = [sb([P, PACK, HALF], F32, "picked0%d" % h) for h in range(2)]
+        picked_late = sb([P, PACK, SLOTS], F32, "picked1")
+
+        def picked(s, c0, c1):
+            if s == 1:
+                return picked_late[:, :, c0:c1]
+            h = c0 // HALF
+            return picked_halves[h][:, :, c0 - h * HALF:c1 - h * HALF]
 
         def entries(j0, j1):
             return own_list[:, j0 // PER_COLUMN:j1 // PER_COLUMN]
@@ -122,28 +130,33 @@ def tile_moe_loc_lin_relu_kernel(tc, x_words, x_scales, xo, w, gate, offs, offs2
         def pick(s, j, c0, c1, on_vector=False):
             window = x_row[s, j].indirect(entries(c0, c1))
             if on_vector:
-                nc.vector.tensor_copy(picked[s][:, j, c0:c1], window)
+                nc.vector.tensor_copy(picked(s, c0, c1)[:, j, :], window)
             else:
-                nc.scalar.activation(picked[s][:, j, c0:c1], window, COPY)
+                nc.scalar.activation(picked(s, c0, c1)[:, j, :], window, COPY)
 
-        def interleave(grouped, rows, j0, j1, on_scalar=False):
+        def interleave(grouped, rows, j0, j1, on_scalar=False, on_gpsimd=False):
             src = rows.rearrange("p j (c i) -> p c j i", i=WALK)[:, :, j0:j1, :]
             dst = grouped.rearrange("p (c i j) -> p c j i", i=WALK, j=PACK)[:, :, j0:j1, :]
-            if on_scalar:
+            if on_gpsimd:
+                nc.gpsimd.tensor_scalar(dst, src, 1.0, 0.0, MULT, ADD)
+            elif on_scalar:
                 nc.scalar.activation(dst, src, COPY)
             else:
                 nc.vector.tensor_copy(dst, src)
 
-        x_grouped = [sb([P, PACK * SLOTS], BF16, "x_grouped%d" % s) for s in range(PASSES)]
+        x_grouped = {(0, 0): sb([P, PACK * HALF], BF16, "x_grouped00")[:]}
+        grouped_late = sb([P, PACK * SLOTS], BF16, "x_grouped1")
+        for h in range(2):
+            x_grouped[1, h] = grouped_late[:, PACK * HALF * h:PACK * HALF * (h + 1)]
         own = {}
 
         def weave_x(s, j0, j1, c0, c1, on_scalar=False):
-            interleave(x_grouped[s][:, PACK * c0:PACK * c1], picked[s][:, :, c0:c1], j0, j1, on_scalar)
+            interleave(x_grouped[s, c0 // HALF], picked(s, c0, c1), j0, j1, on_scalar)
 
         def quantize_x(s, c0, c1, tag=None):
             codes = sb([P, c1 - c0], U32, "own_codes%d_%d" % (s, c0), tag=tag)
             scales = sb([P, c1 - c0], U8, "own_scales%d_%d" % (s, c0))
-            nc.vector.quantize_mx(out=codes[:].bitcast(FP8X4), scales=scales[:], in_=x_grouped[s][:, PACK * c0:PACK * c1])
+            nc.vector.quantize_mx(out=codes[:].bitcast(FP8X4), scales=scales[:], in_=x_grouped[s, c0 // HALF])
             for e in range(c0 // C, c1 // C):
                 cols = slice(e * C - c0, (e + 1) * C - c0)
                 own[e, s] = (codes[:, cols], scales[:, cols])
@@ -204,17 +217,20 @@ def tile_moe_loc_lin_relu_kernel(tc, x_words, x_scales, xo, w, gate, offs, offs2
             pick(s, j, HALF, SLOTS, on_vector=True)
 
         share(0, 0)
-        pick(0, 1, 0, SLOTS)
+        pick(0, 1, 0, HALF)
+        pick(0, 1, HALF, SLOTS)
         share(0, 2)
         share(0, 3)
         gate_sb = sb([P, SLOTS], F32, "gate_sb", tag="x_raw03")
         nc.scalar.activation(gate_sb[:], gate_bank[:], COPY)
-        weave_x(0, 0, 4, 0, SLOTS)
+        weave_x(0, 0, 4, 0, HALF)
+        x_grouped[0, 1] = sb([P, PACK * HALF], BF16, "x_grouped01", tag="picked00")[:]
+        interleave(x_grouped[0, 1], picked(0, HALF, SLOTS), 0, PACK, on_gpsimd=True)
         share(1, 0)
-        quantize_x(0, 0, HALF)
         share(1, 1)
+        quantize_x(0, 0, HALF, tag="x_raw11")
         weave_x(1, 0, 2, 0, HALF)
-        pick(1, 2, 0, SLOTS)
+        share(1, 2)
         pick(1, 3, 0, C, on_vector=True)
         pick(1, 3, C, HALF)
         pick(1, 3, HALF, SLOTS)

from contextlib import ExitStack

import concourse.mybir as mybir
from concourse.masks import make_identity

K, T, Q, E, C, N = 1024, 1024, 768, 4, 128, 256
SLOTS = E * C
FLOPS = 2 * 2 * SLOTS * K * N

F32 = mybir.dt.float32
BF16 = mybir.dt.bfloat16
I32 = mybir.dt.int32
U32 = mybir.dt.uint32
U16 = mybir.dt.uint16
U8 = mybir.dt.uint8
FP8X4 = mybir.dt.float8_e4m3fn_x4
COPY = mybir.ActivationFunctionType.Copy
RELU = mybir.ActivationFunctionType.Relu
MULT = mybir.AluOpType.mult
MAX = mybir.AluOpType.max
ADD = mybir.AluOpType.add

P = 128
PACK = 4
K_PASS = P * PACK
PASSES = K // K_PASS
BLOCKS = N // P
QUADRANTS = 4
SCALE_ROWS = 4
PER_COLUMN = 16
HALF = SLOTS // 2
VECTOR_COLUMNS = ((0, 176), (0, 256), (256, 256))
WALK = 4


def tile_moe_loc_lin_relu_kernel(tc, x_words, x_scales, xo, w, gate, offs, offs2, out):
    nc = tc.nc
    with ExitStack() as ctx:
        lists = ctx.enter_context(tc.tile_pool(name="lists", bufs=1))
        keep = ctx.enter_context(tc.tile_pool(name="keep", bufs=1))
        psum = ctx.enter_context(tc.psum_pool(name="psum", bufs=1))

        def sb(shape, dtype, name, tag=None):
            return keep.tile(shape, dtype, name=name, tag=tag or name, align_bytes=64)

        own_list = lists.tile([P, SLOTS // PER_COLUMN], U16, name="own_list")
        far_list = lists.tile([P, SLOTS // PER_COLUMN], U16, name="far_list")

        far_words = [sb([P, Q], I32, "far_words%d" % s) for s in range(PASSES)]
        far_bytes = sb([P, Q], U8, "far_bytes")
        far_codes = [sb([P, SLOTS], U32, "far_codes%d" % s) for s in range(PASSES)]
        far_scales = sb([P, SLOTS], U8, "far_scales")
        own_out = [sb([P, T], F32, "own_out%d" % b) for b in range(BLOCKS)]

        nc.gpsimd.memset(own_out[0][:], 0.0)
        nc.scalar.activation(own_out[1][:], own_out[0][:], COPY)

        def load_words(s):
            nc.sync.dma_start(out=far_words[s][:], in_=x_words[s].rearrange("p t d -> p (t d)").bitcast(I32))

        x_row = {}

        def load_x(s, j0, j1):
            rows = xo[s * K_PASS:(s + 1) * K_PASS, :].rearrange("(p j) t -> p j t", j=PACK)
            raw = sb([P, j1 - j0, T], F32, "x_raw%d%d" % (s, j0))
            nc.sync.dma_start(out=raw[:], in_=rows[:, j0:j1, :])
            for j in range(j0, j1):
                x_row[s, j] = raw[:, j - j0, :]

        w_raw = {}

        def load_w(e, s):
            w_raw[e, s] = sb([P, PACK, N], F32, "w_raw%d%d" % (e, s))
            nc.sync.dma_start(out=w_raw[e, s][:], in_=w[e, s * K_PASS:(s + 1) * K_PASS, :].rearrange("(p j) n -> p j n", j=PACK))

        def load_scales():
            scale_rows = x_scales.bitcast(I32)
            for q in range(QUADRANTS):
                nc.scalar.dma_start(
                    out=far_bytes[32 * q:32 * q + SCALE_ROWS * PASSES, :].bitcast(I32),
                    in_=scale_rows[:, SCALE_ROWS * q:SCALE_ROWS * (q + 1), :],
                )

        gate_rows = sb([P, C], F32, "gate_rows")
        gate_cols = sb([P, E], F32, "gate_cols")
        nc.vector.memset(gate_rows[:], 0.0)
        identity = sb([P, P], F32, "identity")
        make_identity(nc, identity[:])
        nc.gpsimd.memset(far_bytes[:].bitcast(I32), 0)

        load_words(0)
        nc.sync.dma_start(far_list[:], offs2)
        nc.sync.dma_start(own_list[:], offs)
        load_words(1)
        nc.sync.dma_start(out=gate_rows[:E, :], in_=gate[0].rearrange("(e c) -> e c", e=E))
        load_x(0, 0, 1)
        load_x(0, 1, 2)
        load_scales()
        load_x(0, 2, 3)
        load_x(0, 3, 4)
        for j in range(PACK):
            load_x(1, j, j + 1)
        for e in range(E):
            for s in range(PASSES):
                load_w(e, s)

        turned = psum.tile([P, P], F32, name="turned", tag="gate_bank")
        nc.tensor.transpose(turned[:], gate_rows[:], identity[:])
        nc.scalar.activation(gate_cols[:], turned[:, :E], COPY)
        gate_bank = psum.tile([P, SLOTS], F32, name="gate_bank", tag="gate_bank")
        for e in range(E):
            nc.tensor.transpose(gate_bank[:, e * C:(e + 1) * C], gate_cols[:, e:e + 1].to_broadcast([P, P]), identity[:])

        for s in range(PASSES):
            nc.vector.tensor_copy(far_codes[s][:], far_words[s][:].bitcast(U32).indirect(far_list[:]))
        nc.vector.tensor_copy(far_scales[:], far_bytes[:].indirect(far_list[:]))

        picked_halves = [sb([P, PACK, HALF], F32, "picked0%d" % h) for h in range(2)]
        picked_late = sb([P, PACK, SLOTS], F32, "picked1")

        def picked(s, c0, c1):
            if s == 1:
                return picked_late[:, :, c0:c1]
            h = c0 // HALF
            return picked_halves[h][:, :, c0 - h * HALF:c1 - h * HALF]

        def entries(j0, j1):
            return own_list[:, j0 // PER_COLUMN:j1 // PER_COLUMN]

        def pick(s, j, c0, c1, on_vector=False):
            window = x_row[s, j].indirect(entries(c0, c1))
            if on_vector:
                nc.vector.tensor_copy(picked(s, c0, c1)[:, j, :], window)
            else:
                nc.scalar.activation(picked(s, c0, c1)[:, j, :], window, COPY)

        def interleave(grouped, rows, j0, j1, on_scalar=False, on_gpsimd=False):
            src = rows.rearrange("p j (c i) -> p c j i", i=WALK)[:, :, j0:j1, :]
            dst = grouped.rearrange("p (c i j) -> p c j i", i=WALK, j=PACK)[:, :, j0:j1, :]
            if on_gpsimd:
                nc.gpsimd.tensor_scalar(dst, src, 1.0, 0.0, MULT, ADD)
            elif on_scalar:
                nc.scalar.activation(dst, src, COPY)
            else:
                nc.vector.tensor_copy(dst, src)

        x_grouped = {(0, 0): sb([P, PACK * HALF], BF16, "x_grouped00")[:]}
        grouped_late = sb([P, PACK * SLOTS], BF16, "x_grouped1")
        for h in range(2):
            x_grouped[1, h] = grouped_late[:, PACK * HALF * h:PACK * HALF * (h + 1)]
        own = {}

        def weave_x(s, j0, j1, c0, c1, on_scalar=False):
            interleave(x_grouped[s, c0 // HALF], picked(s, c0, c1), j0, j1, on_scalar)

        def quantize_x(s, c0, c1, tag=None):
            codes = sb([P, c1 - c0], U32, "own_codes%d_%d" % (s, c0), tag=tag)
            scales = sb([P, c1 - c0], U8, "own_scales%d_%d" % (s, c0))
            nc.vector.quantize_mx(out=codes[:].bitcast(FP8X4), scales=scales[:], in_=x_grouped[s, c0 // HALF])
            for e in range(c0 // C, c1 // C):
                cols = slice(e * C - c0, (e + 1) * C - c0)
                own[e, s] = (codes[:, cols], scales[:, cols])

        far = {}
        for e in range(E):
            for s in range(PASSES):
                far[e, s] = (far_codes[s][:, e * C:(e + 1) * C], far_scales[SCALE_ROWS * s:P, e * C:(e + 1) * C])

        w_grouped, w_codes, w_scales = {}, {}, {}

        def cast_w(e, s, n0=0, n1=N, on_scalar=False):
            if (e, s) not in w_grouped:
                w_grouped[e, s] = sb([P, PACK * N], BF16, "w_grouped%d%d" % (e, s))
                w_codes[e, s] = sb([P, N], U32, "w_codes%d%d" % (e, s))
                w_scales[e, s] = sb([P, N], U8, "w_scales%d%d" % (e, s))
            interleave(w_grouped[e, s][:, PACK * n0:PACK * n1], w_raw[e, s][:, :, n0:n1], 0, PACK, on_scalar)

        def quantize_w(e, s, n0=0, n1=N):
            nc.vector.quantize_mx(
                out=w_codes[e, s][:, n0:n1].bitcast(FP8X4),
                scales=w_scales[e, s][:, n0:n1],
                in_=w_grouped[e, s][:, PACK * n0:PACK * n1],
            )

        def multiply(acc, e, s, b, tokens, start, stop):
            cols = slice(b * P, (b + 1) * P)
            nc.tensor.matmul_mx(
                out=acc,
                lhsT=w_codes[e, s][:, cols].bitcast(FP8X4),
                lhsT_scale=w_scales[e, s][:, cols],
                rhs=tokens[e, s][0].bitcast(FP8X4),
                rhs_scale=tokens[e, s][1],
                start=start,
                stop=stop,
            )

        def multiply_bank(bank, e, s, tokens):
            for b in range(BLOCKS):
                multiply(bank[:, b, :], e, s, b, tokens, s == 0 and b == 0, s == PASSES - 1 and b == BLOCKS - 1)

        far_early = sb([P, BLOCKS, HALF], F32, "far_early")

        def finish_far(e, dst, on_vector=False):
            bank = psum.tile([P, BLOCKS, C], F32, name="far_bank%d" % e, tag="bank%d" % e)
            for s in range(PASSES):
                multiply_bank(bank, e, s, far)
            if on_vector:
                nc.vector.tensor_scalar_max(dst, bank[:], 0.0)
            else:
                nc.scalar.activation(dst, bank[:], RELU)

        def window(e, b):
            return own_out[b][:].indirect(entries(e * C, (e + 1) * C))

        def share(s, j):
            pick(s, j, 0, HALF)
            pick(s, j, HALF, SLOTS, on_vector=True)

        share(0, 0)
        pick(0, 1, 0, HALF)
        pick(0, 1, HALF, SLOTS)
        share(0, 2)
        share(0, 3)
        gate_sb = sb([P, SLOTS], F32, "gate_sb", tag="x_raw03")
        nc.scalar.activation(gate_sb[:], gate_bank[:], COPY)
        weave_x(0, 0, 4, 0, HALF)
        x_grouped[0, 1] = sb([P, PACK * HALF], BF16, "x_grouped01", tag="picked00")[:]
        interleave(x_grouped[0, 1], picked(0, HALF, SLOTS), 0, PACK, on_gpsimd=True)
        share(1, 0)
        share(1, 1)
        quantize_x(0, 0, HALF, tag="x_raw11")
        weave_x(1, 0, 2, 0, HALF)
        share(1, 2)
        pick(1, 3, 0, C, on_vector=True)
        pick(1, 3, C, HALF)
        pick(1, 3, HALF, SLOTS)
        weave_x(1, 2, 4, 0, HALF)
        weave_x(1, 0, 4, HALF, SLOTS)
        quantize_x(1, 0, HALF)

        last = E - 1
        out_rows = out.rearrange("(b p) c -> p b c", p=P)
        ys = []
        for e in range(last):
            own_bank = psum.tile([P, BLOCKS, C], F32, name="own_bank%d" % e, tag="bank%d" % e)
            for s in range(PASSES):
                cut = VECTOR_COLUMNS[e][s]
                if cut > 0:
                    cast_w(e, s, 0, cut)
                if cut < N:
                    cast_w(e, s, cut, N, on_scalar=True)
            for s in range(PASSES):
                quantize_w(e, s)
                multiply_bank(own_bank, e, s, own)
            if e == 0:
                quantize_x(1, HALF, SLOTS, tag="w_raw01")
                quantize_x(0, HALF, SLOTS, tag="w_grouped01")
            y = sb([P, BLOCKS, C], F32, "y%d" % e)
            ys.append(y)
            g = gate_sb[:, e * C:(e + 1) * C].unsqueeze(1).to_broadcast([P, BLOCKS, C])
            nc.vector.scalar_tensor_tensor(y[:], own_bank[:], 0.0, g, MAX, MULT)
            for b in range(BLOCKS):
                nc.scalar.activation(window(e, b), y[:, b, :], COPY)
            if e < 2:
                finish_far(e, far_early[:, :, e * C:(e + 1) * C])
        nc.sync.dma_start(out=out_rows[:, :, T:T + HALF], in_=far_early[:])

        cast_w(last, 0)
        quantize_w(last, 0)
        cast_w(last, 1, 0, P)
        cast_w(last, 1, P, N)
        banks = [psum.tile([P, C], F32, name="last_bank%d" % b) for b in range(BLOCKS)]
        for b in range(BLOCKS):
            multiply(banks[b][:], last, 0, b, own, True, False)
        for b in range(BLOCKS):
            quantize_w(last, 1, b * P, (b + 1) * P)
            multiply(banks[b][:], last, 1, b, own, False, True)
        far_late = sb([P, BLOCKS, HALF], F32, "far_late", tag="w_grouped31")
        finish_far(2, far_late[:, :, :C], on_vector=True)
        y = [sb([P, C], F32, "y_last%d" % b) for b in range(BLOCKS)]
        nc.vector.scalar_tensor_tensor(y[0][:], banks[0][:], 0.0, gate_sb[:, last * C:], MAX, MULT)
        nc.scalar.activation(window(last, 0), y[0][:], COPY)
        finish_far(last, far_late[:, :, C:], on_vector=True)
        nc.vector.scalar_tensor_tensor(y[1][:], banks[1][:], 0.0, gate_sb[:, last * C:], MAX, MULT)
        nc.vector.tensor_copy(window(last, 1), y[1][:])
        nc.sync.dma_start(out=out_rows[:, :, T + HALF:], in_=far_late[:])
        nc.scalar.dma_start(out=out_rows[:, 0, :T], in_=own_out[0][:])
        nc.sync.dma_start(out=out_rows[:, 1, :T], in_=own_out[1][:])
